import numpy as np
import ml_dtypes


def mxq(x, axis, fmt="e4m3"):
    dtype, down = {"e4m3": (ml_dtypes.float8_e4m3fn, 7), "e5m2": (ml_dtypes.float8_e5m2, 14)}[fmt]
    v = np.moveaxis(np.asarray(x, np.float32).astype(ml_dtypes.bfloat16).astype(np.float64), axis, -1)
    blocks = v.reshape(v.shape[:-1] + (-1, 32))
    amax = np.abs(blocks).max(-1, keepdims=True)
    byte = np.maximum(np.where(amax > 0, np.frexp(amax)[1] - 1 + 127, 0) - down, 1)
    scale = np.exp2(byte - 127.0)
    codes = (blocks / scale).astype(np.float32).astype(dtype).astype(np.float64)
    return np.moveaxis((codes * scale).reshape(v.shape), -1, axis)


WIDE = False


def mx_kscale(k):
    if not WIDE:
        return np.ones(k)
    levels = np.array([10, -10, 5, -5, 0])
    if k % 512:
        return np.exp2(np.random.permutation(np.resize(levels, k // 32))).repeat(32)
    a = np.empty((k // 512, 16))
    for p in range(k // 512):
        a[p, :8] = np.random.permutation(np.resize(levels, 8))
        for g in range(8):
            far = levels[np.abs(levels - a[p, g]) >= 10]
            a[p, g + 8] = far[np.random.randint(len(far))]
    return np.exp2(a.ravel()).repeat(32)


BF16 = ml_dtypes.bfloat16


def bf(x):
    return np.asarray(x, np.float32).astype(BF16)


def f64(x):
    return np.asarray(x).astype(np.float64)


E2M1 = np.array([0.0, 0.5, 1.0, 1.5, 2.0, 3.0, 4.0, 6.0, -0.0, -0.5, -1.0, -1.5, -2.0, -3.0, -4.0, -6.0])


def pack_weight(w, fmt):
    k, n = w.shape
    w = f64(bf(w)).reshape(k // 32, 32, n)
    amax = np.abs(w).max(1)
    if fmt == "e4m3":
        byte = np.frexp(amax)[1] - 1 + 127 - 7
    else:
        mant, ex = np.frexp(amax / 6.0)
        byte = np.where(mant > 0.5, ex, ex - 1) + 127
    byte = np.clip(np.where(amax > 0, byte, 1), 1, 254)
    scaled = (w * np.exp2(127.0 - byte)[:, None, :]).reshape(k, n).astype(np.float32)
    by_word = np.ascontiguousarray(scaled.reshape(k // 512, 128, 4, n).transpose(0, 1, 3, 2))
    if fmt == "e4m3":
        words = by_word.astype(ml_dtypes.float8_e4m3fn).view(np.uint8)
    else:
        c = by_word.astype(ml_dtypes.float4_e2m1fn).view(np.uint8) & 0xF
        words = c[..., 0::2] | (c[..., 1::2] << 4)
    return np.ascontiguousarray(words), np.ascontiguousarray(byte.astype(np.uint8).reshape(k // 512, 16, n))


def unpack_weight(words, scales, fmt):
    g, p, n, _ = words.shape
    if fmt == "e4m3":
        vals = np.ascontiguousarray(words).view(ml_dtypes.float8_e4m3fn).astype(np.float64)
    else:
        nib = np.empty((g, p, n, 4), np.uint8)
        nib[..., 0::2] = words & 0xF
        nib[..., 1::2] = words >> 4
        vals = E2M1[nib]
    vals = vals * np.repeat(np.exp2(scales.astype(np.float64) - 127.0), 8, axis=1)[..., None]
    return vals.transpose(0, 1, 3, 2).reshape(g * 512, n)
def pack4(w):
    words, scales = pack_weight(w, "e2m1")
    return words.reshape(words.shape[0], 128, -1), scales


def unpack4(words, scales):
    return unpack_weight(words.reshape(words.shape[0], 128, -1, 2), scales, "e2m1")


M, K, N = 768, 1536, 1024


def setup_inputs():
    s = mx_kscale(K)
    pools = []
    for _ in range(3):
        o = np.random.standard_normal((K, N)) / np.sqrt(K)
        lam = np.exp(0.3 * np.random.standard_normal((K // 2, 1)))
        turned = np.concatenate([lam * o[K // 2:], -lam * o[:K // 2]], axis=0)
        pools.append(turned / s[:, None])
    help_words, help_scales = pack4(pools[0])
    truth_words, truth_scales = pack_weight(pools[1], "e4m3")
    return {"v": bf(np.random.standard_normal((M, K)) * s),
            "help_words": help_words, "help_scales": help_scales,
            "truth_words": truth_words, "truth_scales": truth_scales,
            "safe": bf(pools[2])}


def reference(v, help_words, help_scales, truth_words, truth_scales, safe):
    vq = mxq(f64(v), 1, "e4m3")
    a = vq @ unpack4(help_words, help_scales)
    b = vq @ unpack_weight(truth_words, truth_scales, "e4m3")
    c = vq @ mxq(f64(safe), 0, "e4m3")
    z = np.minimum(a + b, c)
    return 1.0 / (1.0 + np.exp(-z))

@@ -1,0 +1,298 @@
+from contextlib import ExitStack
+
+import concourse.mybir as mybir
+from concourse.masks import make_identity
+
+M, K, N = 768, 1536, 1024
+FLOPS = 3 * 2 * M * K * N
+
+F32 = mybir.dt.float32
+BF16 = mybir.dt.bfloat16
+I32 = mybir.dt.int32
+U32 = mybir.dt.uint32
+U8 = mybir.dt.uint8
+FP8X4 = mybir.dt.float8_e4m3fn_x4
+FP4X4 = mybir.dt.float4_e2m1fn_x4
+SIGMOID = mybir.ActivationFunctionType.Sigmoid
+MIN = mybir.AluOpType.min
+
+P = 128
+K_PASS = 512
+GROUPS = K // K_PASS
+M_BLOCKS = M // P
+N_TILE = 512
+N_TILES = N // N_TILE
+BY_TENSOR = (0, 1, 2)
+BY_VECTOR = (3, 4, 5)
+BANKS_ON_VECTOR = (1, 4)
+SAFE_SPLIT = (512, 512, 640)
+IDLE_PASSES = 16
+MOVING_CODES_AT = 64
+STATIONARY_CODES_AT = 192
+STATIONARY_PLANES_AT = 128
+LAST_WIDTHS = (256, 128, 128)
+
+
+def tile_skew_preference_min_s10_kernel(tc, v, help_words, help_scales, truth_words, truth_scales, safe, out):
+    nc = tc.nc
+    with ExitStack() as ctx:
+        keep = ctx.enter_context(tc.tile_pool(name="keep", bufs=1))
+        psum = ctx.enter_context(tc.psum_pool(name="psum", bufs=8))
+        ctx.enter_context(tc.manual_schedule())
+
+        def sbuf(shape, dtype, name):
+            tile = keep.tile(shape, dtype, name=name, align_bytes=256)
+            return tile
+
+        def shifted(width, dtype, name, at):
+            size = 1 if dtype == U8 else 4
+            tile = sbuf([P, at // size + width], dtype, name)
+            return tile[:, at // size :]
+
+        identity = sbuf([P, P], F32, "identity")
+        warm = sbuf([P, 2], F32, "warm")
+        help_planes = sbuf([P, GROUPS, N], U8, "help_planes")
+        truth_planes = sbuf([P, GROUPS, N], U8, "truth_planes")
+        help_codes = shifted(GROUPS * 2 * N, U8, "help_codes", MOVING_CODES_AT)
+        truth_codes = [shifted(4 * N, U8, "truth_codes%d" % g, MOVING_CODES_AT) for g in range(GROUPS)]
+        v_raw = [sbuf([P, K], BF16, "v_raw%d" % m) for m in range(M_BLOCKS)]
+        v_grouped = [sbuf([P, GROUPS * P * 4], BF16, "v_grouped%d" % m) for m in range(M_BLOCKS)]
+        v_codes = [shifted(GROUPS * P, U32, "v_codes%d" % m, STATIONARY_CODES_AT) for m in range(M_BLOCKS)]
+        v_planes = [shifted(GROUPS * P, U8, "v_planes%d" % m, STATIONARY_PLANES_AT) for m in range(M_BLOCKS)]
+        v_sorted = {m: sbuf([P, K // 2], F32, "v_sorted%d" % m) for m in BY_VECTOR}
+        v_turned = {m: sbuf([P, K // 2], F32, "v_turned%d" % m) for m in BY_VECTOR}
+        idle = sbuf([P, K_PASS], BF16, "idle")
+        idle_codes = sbuf([P, P], U32, "idle_codes")
+        idle_planes = sbuf([P, P], U8, "idle_planes")
+        safe_raw = [sbuf([P, 4, N], BF16, "safe_raw%d" % g) for g in range(GROUPS)]
+        safe_grouped = [sbuf([P, N, 4], BF16, "safe_grouped%d" % g) for g in range(GROUPS)]
+        safe_codes = [shifted(N, U32, "safe_codes%d" % g, MOVING_CODES_AT) for g in range(GROUPS)]
+        safe_planes = [sbuf([P, N], U8, "safe_planes%d" % g) for g in range(GROUPS)]
+
+        nc.gpsimd.memset(idle[:], 0.0)
+        nc.vector.quantize_mx(out=idle_codes[:].bitcast(FP8X4), scales=idle_planes[:], in_=idle[:])
+        nc.vector.memset(help_planes[:].rearrange("p g n -> p (g n)").bitcast(I32), 0)
+        nc.vector.memset(warm[:], 0.0)
+        nc.vector.memset(truth_planes[:].rearrange("p g n -> p (g n)").bitcast(I32), 0)
+        make_identity(nc, identity[:])
+
+        def load_v(m, cols):
+            nc.sync.dma_start(out=v_raw[m][:, cols], in_=v[m * P : (m + 1) * P, cols])
+
+        def load_v_quarters(m):
+            source = v[m * P : (m + 1) * P, :].rearrange("(j s) (g x) -> j (s g) x", s=4, g=GROUPS)
+            for a in (0, 2, 1, 3):
+                nc.sync.dma_start(
+                    out=v_raw[m][32 * a : 32 * a + 32, :].rearrange("j (b x) -> j b x", x=P),
+                    in_=source[:, :, a * P : (a + 1) * P],
+                )
+
+        def load_planes(engine, planes, scales, first):
+            for q in range(4):
+                engine.dma_start(
+                    out=planes[32 * q + first : 32 * q + first + 4, :, :].bitcast(I32),
+                    in_=scales[:, 4 * q : 4 * q + 4, :].bitcast(I32).rearrange("g r n -> r g n"),
+                )
+
+        def load_help(first, last):
+            nc.sync.dma_start(
+                out=help_codes[:, first * 2 * N : last * 2 * N].bitcast(I32).rearrange("p (g b) -> p g b", g=last - first),
+                in_=help_words[first:last].rearrange("g p b -> p g b").bitcast(I32),
+            )
+
+        load_v(0, slice(0, K))
+        load_v(1, slice(0, K))
+        load_planes(nc.scalar, help_planes, help_scales, 0)
+        load_v(2, slice(0, K))
+        load_help(0, 1)
+        load_help(1, 3)
+        load_planes(nc.sync, truth_planes, truth_scales, 4)
+        for g in range(GROUPS):
+            nc.sync.dma_start(
+                out=truth_codes[g].bitcast(I32), in_=truth_words[g].rearrange("p n t -> p (n t)").bitcast(I32)
+            )
+        for m in BY_VECTOR:
+            load_v_quarters(m)
+        for g in range(GROUPS):
+            nc.sync.dma_start(
+                out=safe_raw[g][:], in_=safe[g * K_PASS : (g + 1) * K_PASS, :].rearrange("(p t) n -> p t n", t=4)
+            )
+
+        nc.scalar.activation(out=warm[:, 1:2], in_=warm[:, 0:1], func=SIGMOID)
+
+        def quantise_v(m, first, last):
+            nc.vector.quantize_mx(
+                out=v_codes[m][:, first * P : last * P].bitcast(FP8X4),
+                scales=v_planes[m][:, first * P : last * P],
+                in_=v_grouped[m][:, first * K_PASS : last * K_PASS],
+            )
+
+        def turn_on_tensor(blocks):
+            units = [(m, g) for m in blocks for g in range(GROUPS)]
+            waiting = []
+            for b in range((len(units) + 1) // 2):
+                bank = psum.tile([P, 512], F32, name="bank")
+                here = units[2 * b : 2 * b + 2]
+                for q, (m, g) in enumerate(here):
+                    words = v_raw[m][:].bitcast(F32)
+                    for u in range(2):
+                        at = (2 * q + u) * P
+                        nc.tensor.transpose(bank[:, at : at + P], words[:, 256 * g + u : 256 * (g + 1) : 2], identity[:])
+                for q, (m, g) in enumerate(here):
+                    source = bank[:, 256 * q : 256 * (q + 1)].rearrange("p (u r) -> p r u", u=2)
+                    target = v_grouped[m][:, g * K_PASS : (g + 1) * K_PASS].bitcast(F32).rearrange("p (r u) -> p r u", u=2)
+                    if b in BANKS_ON_VECTOR:
+                        nc.vector.tensor_copy(out=target, in_=source)
+                    else:
+                        nc.scalar.copy(out=target, in_=source)
+                for m, g in waiting:
+                    quantise_v(m, g, g + 1)
+                waiting = here
+            for m, g in waiting:
+                quantise_v(m, g, g + 1)
+
+        def turn_on_vector(m):
+            for g in range(GROUPS):
+                nc.vector.tensor_copy(
+                    out=v_sorted[m][:, 256 * g : 256 * (g + 1)].rearrange("p (s u i) -> p s u i", s=4, u=2),
+                    in_=v_raw[m][:].bitcast(F32).rearrange("p (s g i u) -> p g s u i", s=4, g=GROUPS, u=2)[:, g],
+                )
+            for g in range(GROUPS):
+                nc.vector.transpose(
+                    out=v_turned[m][:, 256 * g : 256 * (g + 1)], in_=v_sorted[m][:, 256 * g : 256 * (g + 1)]
+                )
+            for g in range(GROUPS):
+                nc.vector.tensor_copy(
+                    out=v_grouped[m][:, g * K_PASS : (g + 1) * K_PASS]
+                    .bitcast(F32)
+                    .rearrange("p (j h w) -> p h j w", h=2, w=4),
+                    in_=v_turned[m][:, 256 * g : 256 * (g + 1)].rearrange("p (h w j) -> p h j w", h=2, w=4),
+                )
+            quantise_v(m, 0, 2)
+            quantise_v(m, 2, 3)
+
+        def interleave_safe(copy, g, first, last):
+            copy(
+                out=safe_grouped[g][:, first:last, :].rearrange("p (c i) t -> p c t i", i=4),
+                in_=safe_raw[g][:, :, first:last].rearrange("p t (c i) -> p c t i", i=4),
+            )
+
+        def quantise_safe(g, n):
+            cols = slice(n * N_TILE, (n + 1) * N_TILE)
+            nc.vector.quantize_mx(
+                out=safe_codes[g][:, cols].bitcast(FP8X4),
+                scales=safe_planes[g][:, cols],
+                in_=safe_grouped[g][:, cols, :].rearrange("p c t -> p (c t)"),
+            )
+
+        def prepare_safe(g):
+            split = SAFE_SPLIT[g]
+            interleave_safe(nc.vector.tensor_copy, g, 0, 512)
+            interleave_safe(nc.scalar.copy, g, split, N)
+            if split > 512:
+                interleave_safe(nc.vector.tensor_copy, g, 512, split)
+            quantise_safe(g, 0)
+            quantise_safe(g, 1)
+
+        def mx_pass(acc, m, g, rhs, rhs_scale, start, stop):
+            cols = slice(g * P, (g + 1) * P)
+            nc.tensor.matmul_mx(
+                out=acc,
+                lhsT=v_codes[m][:, cols].bitcast(FP8X4),
+                lhsT_scale=v_planes[m][:, cols],
+                rhs=rhs,
+                rhs_scale=rhs_scale,
+                start=start,
+                stop=stop,
+            )
+
+        def help_pass(acc, m, n, g):
+            first = g * 2 * N + n * 1024
+            codes = help_codes[:, first : first + 1024].bitcast(FP4X4)
+            planes = help_planes[:, g, n * N_TILE : (n + 1) * N_TILE]
+            mx_pass(acc[:], m, g, codes, planes, g == 0, False)
+
+        def truth_pass(acc, m, n, g):
+            codes = truth_codes[g][:, n * 2048 : (n + 1) * 2048].bitcast(FP8X4)
+            planes = truth_planes[4:P, g, n * N_TILE : (n + 1) * N_TILE]
+            mx_pass(acc[:], m, g, codes, planes, False, g == GROUPS - 1)
+
+        def safe_pass(acc, m, g, first, width):
+            cols = slice(first, first + width)
+            mx_pass(acc[:, 0:width], m, g, safe_codes[g][:, cols].bitcast(FP8X4), safe_planes[g][:, cols], g == 0, g == GROUPS - 1)
+
+        open_banks = {}
+        sums = {}
+
+        def help_blocks(blocks):
+            tiles = [(m, n) for m in blocks for n in range(N_TILES)]
+            for tile in tiles:
+                bank = psum.tile([P, 512], F32, name="bank")
+                open_banks[tile] = bank
+            for g in range(GROUPS):
+                for m, n in tiles:
+                    help_pass(open_banks[(m, n)], m, n, g)
+
+        def truth_blocks(blocks):
+            for m in blocks:
+                for n in range(N_TILES):
+                    for g in range(GROUPS):
+                        truth_pass(open_banks[(m, n)], m, n, g)
+                    kept = sbuf([P, N_TILE], F32, "sum%d_%d" % (m, n))
+                    nc.scalar.copy(out=kept[:], in_=open_banks[(m, n)][:])
+                    sums[(m, n)] = kept
+
+        def finish(bank, m, n, first, width):
+            low = sums[(m, n)][:, first : first + width]
+            result = sbuf([P, width], F32, "result%d_%d_%d" % (m, n, first))
+            nc.vector.tensor_tensor(out=low, in0=bank[:, 0:width], in1=low, op=MIN)
+            nc.scalar.activation(out=result[:], in_=low, func=SIGMOID)
+            at = n * N_TILE + first
+            nc.sync.dma_start(out=out[m * P : (m + 1) * P, at : at + width], in_=result[:])
+
+        idle_bank = psum.tile([P, 512], F32, name="bank")
+        for i in range(IDLE_PASSES):
+            nc.tensor.matmul_mx(
+                out=idle_bank[:, 0:P],
+                lhsT=idle_codes[:].bitcast(FP8X4),
+                lhsT_scale=idle_planes[:],
+                rhs=idle_codes[:].bitcast(FP8X4),
+                rhs_scale=idle_planes[:],
+                start=True,
+                stop=True,
+            )
+
+        turn_on_tensor(BY_TENSOR)
+        help_blocks(BY_TENSOR)
+        turn_on_vector(3)
+        truth_blocks(BY_TENSOR)
+        turn_on_vector(4)
+        help_blocks((3,))
+        truth_blocks((3,))
+        turn_on_vector(5)
+        prepare_safe(0)
+        help_blocks((4,))
+        truth_blocks((4,))
+        prepare_safe(1)
+        help_blocks((5,))
+        truth_blocks((5,))
+        prepare_safe(2)
+
+        early = [(m, n) for m in BY_TENSOR for n in range(N_TILES)]
+        for tile in early:
+            bank = psum.tile([P, 512], F32, name="bank")
+            open_banks[tile] = bank
+        for g in range(GROUPS):
+            for m, n in early:
+                safe_pass(open_banks[(m, n)], m, g, n * N_TILE, N_TILE)
+                if g == GROUPS - 1:
+                    finish(open_banks[(m, n)], m, n, 0, N_TILE)
+        for m in BY_VECTOR:
+            for n in range(N_TILES):
+                first = 0
+                for width in LAST_WIDTHS if (m, n) == (M_BLOCKS - 1, N_TILES - 1) else (N_TILE,):
+                    bank = psum.tile([P, 512], F32, name="bank")
+                    for g in range(GROUPS):
+                        safe_pass(bank, m, g, n * N_TILE + first, width)
+                    finish(bank, m, n, first, width)
+                    first = first + width

@@ -26,7 +26,6 @@ BY_TENSOR = (0, 1, 2)
 BY_VECTOR = (3, 4, 5)
 BANKS_ON_VECTOR = (1, 4)
 SAFE_SPLIT = (512, 512, 640)
-IDLE_PASSES = 16
 MOVING_CODES_AT = 64
 STATIONARY_CODES_AT = 192
 STATIONARY_PLANES_AT = 128
@@ -50,7 +49,6 @@ def tile_skew_preference_min_s10_kernel(tc, v, help_words, help_scales, truth_wo
             return tile[:, at // size :]
 
         identity = sbuf([P, P], F32, "identity")
-        warm = sbuf([P, 2], F32, "warm")
         help_planes = sbuf([P, GROUPS, N], U8, "help_planes")
         truth_planes = sbuf([P, GROUPS, N], U8, "truth_planes")
         help_codes = shifted(GROUPS * 2 * N, U8, "help_codes", MOVING_CODES_AT)
@@ -61,18 +59,12 @@ def tile_skew_preference_min_s10_kernel(tc, v, help_words, help_scales, truth_wo
         v_planes = [shifted(GROUPS * P, U8, "v_planes%d" % m, STATIONARY_PLANES_AT) for m in range(M_BLOCKS)]
         v_sorted = {m: sbuf([P, K // 2], F32, "v_sorted%d" % m) for m in BY_VECTOR}
         v_turned = {m: sbuf([P, K // 2], F32, "v_turned%d" % m) for m in BY_VECTOR}
-        idle = sbuf([P, K_PASS], BF16, "idle")
-        idle_codes = sbuf([P, P], U32, "idle_codes")
-        idle_planes = sbuf([P, P], U8, "idle_planes")
         safe_raw = [sbuf([P, 4, N], BF16, "safe_raw%d" % g) for g in range(GROUPS)]
         safe_grouped = [sbuf([P, N, 4], BF16, "safe_grouped%d" % g) for g in range(GROUPS)]
         safe_codes = [shifted(N, U32, "safe_codes%d" % g, MOVING_CODES_AT) for g in range(GROUPS)]
         safe_planes = [sbuf([P, N], U8, "safe_planes%d" % g) for g in range(GROUPS)]
 
-        nc.gpsimd.memset(idle[:], 0.0)
-        nc.vector.quantize_mx(out=idle_codes[:].bitcast(FP8X4), scales=idle_planes[:], in_=idle[:])
         nc.vector.memset(help_planes[:].rearrange("p g n -> p (g n)").bitcast(I32), 0)
-        nc.vector.memset(warm[:], 0.0)
         nc.vector.memset(truth_planes[:].rearrange("p g n -> p (g n)").bitcast(I32), 0)
         make_identity(nc, identity[:])
 
@@ -117,8 +109,6 @@ def tile_skew_preference_min_s10_kernel(tc, v, help_words, help_scales, truth_wo
             nc.sync.dma_start(
                 out=safe_raw[g][:], in_=safe[g * K_PASS : (g + 1) * K_PASS, :].rearrange("(p t) n -> p t n", t=4)
             )
-
-        nc.scalar.activation(out=warm[:, 1:2], in_=warm[:, 0:1], func=SIGMOID)
 
         def quantise_v(m, first, last):
             nc.vector.quantize_mx(
@@ -249,18 +239,6 @@ def tile_skew_preference_min_s10_kernel(tc, v, help_words, help_scales, truth_wo
             nc.scalar.activation(out=result[:], in_=low, func=SIGMOID)
             at = n * N_TILE + first
             nc.sync.dma_start(out=out[m * P : (m + 1) * P, at : at + width], in_=result[:])
-
-        idle_bank = psum.tile([P, 512], F32, name="bank")
-        for i in range(IDLE_PASSES):
-            nc.tensor.matmul_mx(
-                out=idle_bank[:, 0:P],
-                lhsT=idle_codes[:].bitcast(FP8X4),
-                lhsT_scale=idle_planes[:],
-                rhs=idle_codes[:].bitcast(FP8X4),
-                rhs_scale=idle_planes[:],
-                start=True,
-                stop=True,
-            )
 
         turn_on_tensor(BY_TENSOR)
         help_blocks(BY_TENSOR)

@@ -22,21 +22,23 @@ GROUPS = K // K_PASS
 M_BLOCKS = M // P
 N_TILE = 512
 N_TILES = N // N_TILE
+BANKS = 8
 BY_TENSOR = (0, 1, 2)
 BY_VECTOR = (3, 4, 5)
-BANKS_ON_VECTOR = (1, 4)
-SAFE_SPLIT = (512, 512, 640)
 MOVING_CODES_AT = 64
 STATIONARY_CODES_AT = 192
 STATIONARY_PLANES_AT = 128
-LAST_WIDTHS = (256, 128, 128)
+TRUTH_PLANE_ROW = 4
+SWEEP = 2
+LAST_SPLIT = 256
+PIECES = {(4, 1): (256, 256), (5, 1): (256, 128, 128)}
 
 
 def tile_skew_preference_min_s10_kernel(tc, v, help_words, help_scales, truth_words, truth_scales, safe, out):
     nc = tc.nc
     with ExitStack() as ctx:
         keep = ctx.enter_context(tc.tile_pool(name="keep", bufs=1))
-        psum = ctx.enter_context(tc.psum_pool(name="psum", bufs=8))
+        psum = ctx.enter_context(tc.psum_pool(name="psum", bufs=1))
         ctx.enter_context(tc.manual_schedule())
 
         def sbuf(shape, dtype, name):
@@ -48,30 +50,50 @@ def tile_skew_preference_min_s10_kernel(tc, v, help_words, help_scales, truth_wo
             tile = sbuf([P, at // size + width], dtype, name)
             return tile[:, at // size :]
 
+        taken = []
+
+        def next_bank():
+            bank = psum.tile([P, N_TILE], F32, name="bank%d" % (len(taken) % BANKS))
+            taken.append(bank)
+            return bank
+
+        head = len(BY_TENSOR)
         identity = sbuf([P, P], F32, "identity")
         help_planes = sbuf([P, GROUPS, N], U8, "help_planes")
         truth_planes = sbuf([P, GROUPS, N], U8, "truth_planes")
-        help_codes = shifted(GROUPS * 2 * N, U8, "help_codes", MOVING_CODES_AT)
+        help_codes = [shifted(2 * N, U8, "help_codes%d" % g, MOVING_CODES_AT) for g in range(GROUPS)]
         truth_codes = [shifted(4 * N, U8, "truth_codes%d" % g, MOVING_CODES_AT) for g in range(GROUPS)]
-        v_raw = [sbuf([P, K], BF16, "v_raw%d" % m) for m in range(M_BLOCKS)]
-        v_grouped = [sbuf([P, GROUPS * P * 4], BF16, "v_grouped%d" % m) for m in range(M_BLOCKS)]
-        v_codes = [shifted(GROUPS * P, U32, "v_codes%d" % m, STATIONARY_CODES_AT) for m in range(M_BLOCKS)]
-        v_planes = [shifted(GROUPS * P, U8, "v_planes%d" % m, STATIONARY_PLANES_AT) for m in range(M_BLOCKS)]
+        units = [(m, g) for g in range(GROUPS) for m in BY_TENSOR]
+        head_loads = [units[0:1], units[1:head]] + [units[g * head : (g + 1) * head] for g in range(1, GROUPS)]
+        head_raw = [sbuf([P, len(load) * K_PASS], BF16, "head_raw%d" % i) for i, load in enumerate(head_loads)]
+        head_grouped = sbuf([P, len(units) * K_PASS], BF16, "head_grouped")
+        head_codes = shifted(len(units) * P, U32, "head_codes", STATIONARY_CODES_AT)
+        head_planes = shifted(len(units) * P, U8, "head_planes", STATIONARY_PLANES_AT)
+        v_raw = {m: sbuf([P, K], BF16, "v_raw%d" % m) for m in BY_VECTOR}
         v_sorted = {m: sbuf([P, K // 2], F32, "v_sorted%d" % m) for m in BY_VECTOR}
         v_turned = {m: sbuf([P, K // 2], F32, "v_turned%d" % m) for m in BY_VECTOR}
+        v_grouped = {m: sbuf([P, K], BF16, "v_grouped%d" % m) for m in BY_VECTOR}
+        v_codes = {m: shifted(GROUPS * P, U32, "v_codes%d" % m, STATIONARY_CODES_AT) for m in BY_VECTOR}
+        v_planes = {m: shifted(GROUPS * P, U8, "v_planes%d" % m, STATIONARY_PLANES_AT) for m in BY_VECTOR}
         safe_raw = [sbuf([P, 4, N], BF16, "safe_raw%d" % g) for g in range(GROUPS)]
-        safe_grouped = [sbuf([P, N, 4], BF16, "safe_grouped%d" % g) for g in range(GROUPS)]
-        safe_codes = [shifted(N, U32, "safe_codes%d" % g, MOVING_CODES_AT) for g in range(GROUPS)]
-        safe_planes = [sbuf([P, N], U8, "safe_planes%d" % g) for g in range(GROUPS)]
+        halves = [(g, n) for g in range(GROUPS) for n in range(N_TILES)]
+        safe_grouped = {h: sbuf([P, N_TILE, 4], BF16, "safe_grouped%d_%d" % h) for h in halves}
+        safe_codes = {h: shifted(N_TILE, U32, "safe_codes%d_%d" % h, MOVING_CODES_AT) for h in halves}
+        safe_planes = {h: sbuf([P, N_TILE], U8, "safe_planes%d_%d" % h) for h in halves}
 
         nc.vector.memset(help_planes[:].rearrange("p g n -> p (g n)").bitcast(I32), 0)
         nc.vector.memset(truth_planes[:].rearrange("p g n -> p (g n)").bitcast(I32), 0)
         make_identity(nc, identity[:])
 
-        def load_v(m, cols):
-            nc.sync.dma_start(out=v_raw[m][:, cols], in_=v[m * P : (m + 1) * P, cols])
+        def load_head(i):
+            first, g = head_loads[i][0]
+            count = len(head_loads[i])
+            nc.sync.dma_start(
+                out=head_raw[i][:].rearrange("p (m x) -> p m x", m=count),
+                in_=v[first * P : (first + count) * P, g * K_PASS : (g + 1) * K_PASS].rearrange("(m p) x -> p m x", p=P),
+            )
 
-        def load_v_quarters(m):
+        def load_quarters(m):
             source = v[m * P : (m + 1) * P, :].rearrange("(j s) (g x) -> j (s g) x", s=4, g=GROUPS)
             for a in (0, 2, 1, 3):
                 nc.sync.dma_start(
@@ -79,198 +101,208 @@ def tile_skew_preference_min_s10_kernel(tc, v, help_words, help_scales, truth_wo
                     in_=source[:, :, a * P : (a + 1) * P],
                 )
 
-        def load_planes(engine, planes, scales, first):
-            for q in range(4):
-                engine.dma_start(
-                    out=planes[32 * q + first : 32 * q + first + 4, :, :].bitcast(I32),
-                    in_=scales[:, 4 * q : 4 * q + 4, :].bitcast(I32).rearrange("g r n -> r g n"),
-                )
+        def load_planes(planes, scales, first):
+            by_row = scales.bitcast(I32).rearrange("g (q r) n -> r q g n", r=4)
+            for r in range(4):
+                nc.sync.dma_start(out=planes[first + r : P : 32, :, :].bitcast(I32), in_=by_row[r])
 
-        def load_help(first, last):
-            nc.sync.dma_start(
-                out=help_codes[:, first * 2 * N : last * 2 * N].bitcast(I32).rearrange("p (g b) -> p g b", g=last - first),
-                in_=help_words[first:last].rearrange("g p b -> p g b").bitcast(I32),
-            )
+        def load_help(g):
+            nc.sync.dma_start(out=help_codes[g].bitcast(I32), in_=help_words[g].bitcast(I32))
 
-        load_v(0, slice(0, K))
-        load_v(1, slice(0, K))
-        load_planes(nc.scalar, help_planes, help_scales, 0)
-        load_v(2, slice(0, K))
-        load_help(0, 1)
-        load_help(1, 3)
-        load_planes(nc.sync, truth_planes, truth_scales, 4)
-        for g in range(GROUPS):
+        def load_truth(g):
             nc.sync.dma_start(
                 out=truth_codes[g].bitcast(I32), in_=truth_words[g].rearrange("p n t -> p (n t)").bitcast(I32)
             )
-        for m in BY_VECTOR:
-            load_v_quarters(m)
-        for g in range(GROUPS):
+
+        def load_safe(g):
             nc.sync.dma_start(
                 out=safe_raw[g][:], in_=safe[g * K_PASS : (g + 1) * K_PASS, :].rearrange("(p t) n -> p t n", t=4)
             )
 
-        def quantise_v(m, first, last):
+        for i in range(len(head_loads)):
+            load_head(i)
+        load_planes(help_planes, help_scales, 0)
+        for g in range(GROUPS):
+            load_help(g)
+        load_truth(0)
+        load_planes(truth_planes, truth_scales, TRUTH_PLANE_ROW)
+        load_truth(1)
+        load_truth(2)
+        for m in BY_VECTOR:
+            load_quarters(m)
+        for g in range(GROUPS):
+            load_safe(g)
+
+        head_words = {}
+        for i, load in enumerate(head_loads):
+            for q, unit in enumerate(load):
+                head_words[unit] = head_raw[i][:].bitcast(F32)[:, 256 * q : 256 * (q + 1)]
+
+        def turn_on_tensor(first, last):
+            bank = next_bank()
+            count = last - first
+            for q, unit in enumerate(units[first:last]):
+                for u in range(2):
+                    at = (2 * q + u) * P
+                    nc.tensor.transpose(bank[:, at : at + P], head_words[unit][:, u:256:2], identity[:])
+            grouped = head_grouped[:, first * K_PASS : last * K_PASS]
+            nc.scalar.copy(
+                out=grouped.bitcast(F32).rearrange("p (q r u) -> p q r u", q=count, u=2),
+                in_=bank[:, 0 : count * 256].rearrange("p (q u r) -> p q r u", q=count, u=2),
+            )
             nc.vector.quantize_mx(
-                out=v_codes[m][:, first * P : last * P].bitcast(FP8X4),
-                scales=v_planes[m][:, first * P : last * P],
-                in_=v_grouped[m][:, first * K_PASS : last * K_PASS],
+                out=head_codes[:, first * P : last * P].bitcast(FP8X4), scales=head_planes[:, first * P : last * P], in_=grouped
             )
 
-        def turn_on_tensor(blocks):
-            units = [(m, g) for m in blocks for g in range(GROUPS)]
-            waiting = []
-            for b in range((len(units) + 1) // 2):
-                bank = psum.tile([P, 512], F32, name="bank")
-                here = units[2 * b : 2 * b + 2]
-                for q, (m, g) in enumerate(here):
-                    words = v_raw[m][:].bitcast(F32)
-                    for u in range(2):
-                        at = (2 * q + u) * P
-                        nc.tensor.transpose(bank[:, at : at + P], words[:, 256 * g + u : 256 * (g + 1) : 2], identity[:])
-                for q, (m, g) in enumerate(here):
-                    source = bank[:, 256 * q : 256 * (q + 1)].rearrange("p (u r) -> p r u", u=2)
-                    target = v_grouped[m][:, g * K_PASS : (g + 1) * K_PASS].bitcast(F32).rearrange("p (r u) -> p r u", u=2)
-                    if b in BANKS_ON_VECTOR:
-                        nc.vector.tensor_copy(out=target, in_=source)
-                    else:
-                        nc.scalar.copy(out=target, in_=source)
-                for m, g in waiting:
-                    quantise_v(m, g, g + 1)
-                waiting = here
-            for m, g in waiting:
-                quantise_v(m, g, g + 1)
+        def sort_words(m, g):
+            nc.vector.tensor_copy(
+                out=v_sorted[m][:, 256 * g : 256 * (g + 1)].rearrange("p (s u i) -> p s u i", s=4, u=2),
+                in_=v_raw[m][:].bitcast(F32).rearrange("p (s g i u) -> p g s u i", s=4, g=GROUPS, u=2)[:, g],
+            )
+
+        def turn_squares(m, g):
+            nc.vector.transpose(out=v_turned[m][:, 256 * g : 256 * (g + 1)], in_=v_sorted[m][:, 256 * g : 256 * (g + 1)])
+
+        def pair_words(m, g):
+            nc.vector.tensor_copy(
+                out=v_grouped[m][:, g * K_PASS : (g + 1) * K_PASS].bitcast(F32).rearrange("p (j h w) -> p h j w", h=2, w=4),
+                in_=v_turned[m][:, 256 * g : 256 * (g + 1)].rearrange("p (h w j) -> p h j w", h=2, w=4),
+            )
+
+        def quantise_v(m, g):
+            nc.vector.quantize_mx(
+                out=v_codes[m][:, g * P : (g + 1) * P].bitcast(FP8X4),
+                scales=v_planes[m][:, g * P : (g + 1) * P],
+                in_=v_grouped[m][:, g * K_PASS : (g + 1) * K_PASS],
+            )
 
         def turn_on_vector(m):
-            for g in range(GROUPS):
-                nc.vector.tensor_copy(
-                    out=v_sorted[m][:, 256 * g : 256 * (g + 1)].rearrange("p (s u i) -> p s u i", s=4, u=2),
-                    in_=v_raw[m][:].bitcast(F32).rearrange("p (s g i u) -> p g s u i", s=4, g=GROUPS, u=2)[:, g],
-                )
-            for g in range(GROUPS):
-                nc.vector.transpose(
-                    out=v_turned[m][:, 256 * g : 256 * (g + 1)], in_=v_sorted[m][:, 256 * g : 256 * (g + 1)]
-                )
-            for g in range(GROUPS):
-                nc.vector.tensor_copy(
-                    out=v_grouped[m][:, g * K_PASS : (g + 1) * K_PASS]
-                    .bitcast(F32)
-                    .rearrange("p (j h w) -> p h j w", h=2, w=4),
-                    in_=v_turned[m][:, 256 * g : 256 * (g + 1)].rearrange("p (h w j) -> p h j w", h=2, w=4),
-                )
-            quantise_v(m, 0, 2)
-            quantise_v(m, 2, 3)
+            for step in (sort_words, turn_squares, pair_words, quantise_v):
+                for g in range(GROUPS):
+                    step(m, g)
 
-        def interleave_safe(copy, g, first, last):
+        def stationary(m, g):
+            if m in BY_TENSOR:
+                at = units.index((m, g)) * P
+                return head_codes[:, at : at + P], head_planes[:, at : at + P]
+            return v_codes[m][:, g * P : (g + 1) * P], v_planes[m][:, g * P : (g + 1) * P]
+
+        def interleave_safe(copy, g, n, first, last):
+            at = n * N_TILE
             copy(
-                out=safe_grouped[g][:, first:last, :].rearrange("p (c i) t -> p c t i", i=4),
-                in_=safe_raw[g][:, :, first:last].rearrange("p t (c i) -> p c t i", i=4),
+                out=safe_grouped[(g, n)][:, first:last, :].rearrange("p (c i) t -> p c t i", i=4),
+                in_=safe_raw[g][:, :, at + first : at + last].rearrange("p t (c i) -> p c t i", i=4),
             )
 
         def quantise_safe(g, n):
-            cols = slice(n * N_TILE, (n + 1) * N_TILE)
             nc.vector.quantize_mx(
-                out=safe_codes[g][:, cols].bitcast(FP8X4),
-                scales=safe_planes[g][:, cols],
-                in_=safe_grouped[g][:, cols, :].rearrange("p c t -> p (c t)"),
+                out=safe_codes[(g, n)].bitcast(FP8X4),
+                scales=safe_planes[(g, n)][:],
+                in_=safe_grouped[(g, n)][:].rearrange("p c t -> p (c t)"),
             )
-
-        def prepare_safe(g):
-            split = SAFE_SPLIT[g]
-            interleave_safe(nc.vector.tensor_copy, g, 0, 512)
-            interleave_safe(nc.scalar.copy, g, split, N)
-            if split > 512:
-                interleave_safe(nc.vector.tensor_copy, g, 512, split)
-            quantise_safe(g, 0)
-            quantise_safe(g, 1)
 
         def mx_pass(acc, m, g, rhs, rhs_scale, start, stop):
-            cols = slice(g * P, (g + 1) * P)
+            codes, planes = stationary(m, g)
             nc.tensor.matmul_mx(
-                out=acc,
-                lhsT=v_codes[m][:, cols].bitcast(FP8X4),
-                lhsT_scale=v_planes[m][:, cols],
-                rhs=rhs,
-                rhs_scale=rhs_scale,
-                start=start,
-                stop=stop,
+                out=acc, lhsT=codes.bitcast(FP8X4), lhsT_scale=planes, rhs=rhs, rhs_scale=rhs_scale, start=start, stop=stop
             )
 
-        def help_pass(acc, m, n, g):
-            first = g * 2 * N + n * 1024
-            codes = help_codes[:, first : first + 1024].bitcast(FP4X4)
+        quality_banks = {}
+        quality = {}
+
+        def help_pass(m, n, g):
+            if g == 0:
+                quality_banks[(m, n)] = next_bank()
+            codes = help_codes[g][:, n * 1024 : (n + 1) * 1024].bitcast(FP4X4)
             planes = help_planes[:, g, n * N_TILE : (n + 1) * N_TILE]
-            mx_pass(acc[:], m, g, codes, planes, g == 0, False)
+            mx_pass(quality_banks[(m, n)][:], m, g, codes, planes, g == 0, False)
 
-        def truth_pass(acc, m, n, g):
+        def truth_pass(m, n, g):
             codes = truth_codes[g][:, n * 2048 : (n + 1) * 2048].bitcast(FP8X4)
-            planes = truth_planes[4:P, g, n * N_TILE : (n + 1) * N_TILE]
-            mx_pass(acc[:], m, g, codes, planes, False, g == GROUPS - 1)
+            planes = truth_planes[TRUTH_PLANE_ROW:P, g, n * N_TILE : (n + 1) * N_TILE]
+            mx_pass(quality_banks[(m, n)][:], m, g, codes, planes, False, g == GROUPS - 1)
 
-        def safe_pass(acc, m, g, first, width):
-            cols = slice(first, first + width)
-            mx_pass(acc[:, 0:width], m, g, safe_codes[g][:, cols].bitcast(FP8X4), safe_planes[g][:, cols], g == 0, g == GROUPS - 1)
+        def empty_quality(m, n):
+            kept = sbuf([P, N_TILE], F32, "quality%d_%d" % (m, n))
+            nc.scalar.copy(out=kept[:], in_=quality_banks[(m, n)][:])
+            quality[(m, n)] = kept
 
-        open_banks = {}
-        sums = {}
+        def sweep(one_pass, blocks, groups):
+            for g in groups:
+                for m in blocks:
+                    for n in range(N_TILES):
+                        one_pass(m, n, g)
 
-        def help_blocks(blocks):
-            tiles = [(m, n) for m in blocks for n in range(N_TILES)]
-            for tile in tiles:
-                bank = psum.tile([P, 512], F32, name="bank")
-                open_banks[tile] = bank
+        def quality_tile(m, n):
             for g in range(GROUPS):
-                for m, n in tiles:
-                    help_pass(open_banks[(m, n)], m, n, g)
+                help_pass(m, n, g)
+            for g in range(GROUPS):
+                truth_pass(m, n, g)
 
-        def truth_blocks(blocks):
-            for m in blocks:
-                for n in range(N_TILES):
-                    for g in range(GROUPS):
-                        truth_pass(open_banks[(m, n)], m, n, g)
-                    kept = sbuf([P, N_TILE], F32, "sum%d_%d" % (m, n))
-                    nc.scalar.copy(out=kept[:], in_=open_banks[(m, n)][:])
-                    sums[(m, n)] = kept
+        def safe_pass(bank, m, n, g, first, width):
+            cols = slice(first, first + width)
+            codes = safe_codes[(g, n)][:, cols].bitcast(FP8X4)
+            mx_pass(bank[:, 0:width], m, g, codes, safe_planes[(g, n)][:, cols], g == 0, g == GROUPS - 1)
 
         def finish(bank, m, n, first, width):
-            low = sums[(m, n)][:, first : first + width]
+            low = quality[(m, n)][:, first : first + width]
             result = sbuf([P, width], F32, "result%d_%d_%d" % (m, n, first))
             nc.vector.tensor_tensor(out=low, in0=bank[:, 0:width], in1=low, op=MIN)
             nc.scalar.activation(out=result[:], in_=low, func=SIGMOID)
             at = n * N_TILE + first
             nc.sync.dma_start(out=out[m * P : (m + 1) * P, at : at + width], in_=result[:])
 
-        turn_on_tensor(BY_TENSOR)
-        help_blocks(BY_TENSOR)
-        turn_on_vector(3)
-        truth_blocks(BY_TENSOR)
-        turn_on_vector(4)
-        help_blocks((3,))
-        truth_blocks((3,))
-        turn_on_vector(5)
-        prepare_safe(0)
-        help_blocks((4,))
-        truth_blocks((4,))
-        prepare_safe(1)
-        help_blocks((5,))
-        truth_blocks((5,))
-        prepare_safe(2)
+        def safety_tile(m, n, first, width):
+            bank = next_bank()
+            for g in range(GROUPS):
+                safe_pass(bank, m, n, g, first, width)
+            finish(bank, m, n, first, width)
 
-        early = [(m, n) for m in BY_TENSOR for n in range(N_TILES)]
-        for tile in early:
-            bank = psum.tile([P, 512], F32, name="bank")
-            open_banks[tile] = bank
-        for g in range(GROUPS):
-            for m, n in early:
-                safe_pass(open_banks[(m, n)], m, g, n * N_TILE, N_TILE)
-                if g == GROUPS - 1:
-                    finish(open_banks[(m, n)], m, n, 0, N_TILE)
+        every_group = range(GROUPS)
+        for first in range(0, len(units), 2):
+            turn_on_tensor(first, min(first + 2, len(units)))
+        sweep(help_pass, BY_TENSOR, every_group)
+        sweep(truth_pass, BY_TENSOR, (0,))
         for m in BY_VECTOR:
+            turn_on_vector(m)
+        for m in BY_TENSOR:
             for n in range(N_TILES):
-                first = 0
-                for width in LAST_WIDTHS if (m, n) == (M_BLOCKS - 1, N_TILES - 1) else (N_TILE,):
-                    bank = psum.tile([P, 512], F32, name="bank")
-                    for g in range(GROUPS):
-                        safe_pass(bank, m, g, n * N_TILE + first, width)
-                    finish(bank, m, n, first, width)
-                    first = first + width
+                truth_pass(m, n, 1)
+                truth_pass(m, n, 2)
+                empty_quality(m, n)
+
+        on_vector = nc.vector.tensor_copy
+        interleave_safe(nc.scalar.copy, 0, 1, 0, N_TILE)
+        interleave_safe(on_vector, 0, 0, 0, N_TILE)
+        for n in range(N_TILES):
+            quality_tile(3, n)
+            empty_quality(3, n)
+        interleave_safe(nc.scalar.copy, 1, 1, 0, N_TILE)
+        interleave_safe(on_vector, 1, 0, 0, N_TILE)
+        quantise_safe(0, 0)
+        quantise_safe(1, 0)
+        interleave_safe(on_vector, 2, 0, 0, N_TILE)
+        quantise_safe(0, 1)
+        quantise_safe(2, 0)
+        interleave_safe(on_vector, 2, 1, 0, LAST_SPLIT)
+        quantise_safe(1, 1)
+        for m, n in ((4, 0), (4, 1), (5, 0)):
+            quality_tile(m, n)
+            empty_quality(m, n)
+        interleave_safe(nc.scalar.copy, 2, 1, LAST_SPLIT, N_TILE)
+        quantise_safe(2, 1)
+        quality_tile(5, 1)
+        empty_quality(5, 1)
+
+        banks = [next_bank() for m in range(SWEEP)]
+        for g in every_group:
+            for m in range(SWEEP):
+                safe_pass(banks[m], m, 0, g, 0, N_TILE)
+        for m in range(SWEEP):
+            finish(banks[m], m, 0, 0, N_TILE)
+        rest = [(m, 0) for m in range(SWEEP, M_BLOCKS)] + [(m, 1) for m in range(M_BLOCKS)]
+        for m, n in rest:
+            first = 0
+            for width in PIECES.get((m, n), (N_TILE,)):
+                safety_tile(m, n, first, width)
+                first = first + width

@@ -31,7 +31,6 @@ STATIONARY_PLANES_AT = 128
 TRUTH_PLANE_ROW = 4
 SWEEP = 2
 LAST_SPLIT = 256
-PIECES = {(4, 1): (256, 256), (5, 1): (256, 128, 128)}
 
 
 def tile_skew_preference_min_s10_kernel(tc, v, help_words, help_scales, truth_words, truth_scales, safe, out):
@@ -57,14 +56,16 @@ def tile_skew_preference_min_s10_kernel(tc, v, help_words, help_scales, truth_wo
             taken.append(bank)
             return bank
 
-        head = len(BY_TENSOR)
         identity = sbuf([P, P], F32, "identity")
-        help_planes = sbuf([P, GROUPS, N], U8, "help_planes")
+        help_first = sbuf([P, 1, N], U8, "help_first")
+        help_later = sbuf([P, GROUPS - 1, N], U8, "help_later")
+        help_planes = [help_first[:, 0, :]] + [help_later[:, g, :] for g in range(GROUPS - 1)]
         truth_planes = sbuf([P, GROUPS, N], U8, "truth_planes")
-        help_codes = [shifted(2 * N, U8, "help_codes%d" % g, MOVING_CODES_AT) for g in range(GROUPS)]
+        help_all = shifted(GROUPS * 2 * N, U8, "help_all", MOVING_CODES_AT)
+        help_codes = [help_all[:, g * 2 * N : (g + 1) * 2 * N] for g in range(GROUPS)]
         truth_codes = [shifted(4 * N, U8, "truth_codes%d" % g, MOVING_CODES_AT) for g in range(GROUPS)]
-        units = [(m, g) for g in range(GROUPS) for m in BY_TENSOR]
-        head_loads = [units[0:1], units[1:head]] + [units[g * head : (g + 1) * head] for g in range(1, GROUPS)]
+        units = [(m, g) for m in BY_TENSOR for g in range(GROUPS)]
+        head_loads = [units[0:1], units[1:GROUPS]] + [units[m * GROUPS : (m + 1) * GROUPS] for m in BY_TENSOR[1:]]
         head_raw = [sbuf([P, len(load) * K_PASS], BF16, "head_raw%d" % i) for i, load in enumerate(head_loads)]
         head_grouped = sbuf([P, len(units) * K_PASS], BF16, "head_grouped")
         head_codes = shifted(len(units) * P, U32, "head_codes", STATIONARY_CODES_AT)
@@ -81,17 +82,14 @@ def tile_skew_preference_min_s10_kernel(tc, v, help_words, help_scales, truth_wo
         safe_codes = {h: shifted(N_TILE, U32, "safe_codes%d_%d" % h, MOVING_CODES_AT) for h in halves}
         safe_planes = {h: sbuf([P, N_TILE], U8, "safe_planes%d_%d" % h) for h in halves}
 
-        nc.vector.memset(help_planes[:].rearrange("p g n -> p (g n)").bitcast(I32), 0)
-        nc.vector.memset(truth_planes[:].rearrange("p g n -> p (g n)").bitcast(I32), 0)
+        for planes in (help_first, help_later, truth_planes):
+            nc.vector.memset(planes[:].rearrange("p g n -> p (g n)").bitcast(I32), 0)
         make_identity(nc, identity[:])
 
         def load_head(i):
-            first, g = head_loads[i][0]
-            count = len(head_loads[i])
-            nc.sync.dma_start(
-                out=head_raw[i][:].rearrange("p (m x) -> p m x", m=count),
-                in_=v[first * P : (first + count) * P, g * K_PASS : (g + 1) * K_PASS].rearrange("(m p) x -> p m x", p=P),
-            )
+            m, first = head_loads[i][0]
+            last = first + len(head_loads[i])
+            nc.sync.dma_start(out=head_raw[i][:], in_=v[m * P : (m + 1) * P, first * K_PASS : last * K_PASS])
 
         def load_quarters(m):
             source = v[m * P : (m + 1) * P, :].rearrange("(j s) (g x) -> j (s g) x", s=4, g=GROUPS)
@@ -101,13 +99,16 @@ def tile_skew_preference_min_s10_kernel(tc, v, help_words, help_scales, truth_wo
                     in_=source[:, :, a * P : (a + 1) * P],
                 )
 
-        def load_planes(planes, scales, first):
-            by_row = scales.bitcast(I32).rearrange("g (q r) n -> r q g n", r=4)
+        def load_planes(planes, scales, row, first, last):
+            by_row = scales[first:last].bitcast(I32).rearrange("g (q r) n -> r q g n", r=4)
             for r in range(4):
-                nc.sync.dma_start(out=planes[first + r : P : 32, :, :].bitcast(I32), in_=by_row[r])
+                nc.sync.dma_start(out=planes[row + r : P : 32, :, :].bitcast(I32), in_=by_row[r])
 
-        def load_help(g):
-            nc.sync.dma_start(out=help_codes[g].bitcast(I32), in_=help_words[g].bitcast(I32))
+        def load_help(first, last):
+            nc.sync.dma_start(
+                out=help_all[:, first * 2 * N : last * 2 * N].bitcast(I32).rearrange("p (g b) -> p g b", g=last - first),
+                in_=help_words[first:last].rearrange("g p b -> p g b").bitcast(I32),
+            )
 
         def load_truth(g):
             nc.sync.dma_start(
@@ -121,11 +122,12 @@ def tile_skew_preference_min_s10_kernel(tc, v, help_words, help_scales, truth_wo
 
         for i in range(len(head_loads)):
             load_head(i)
-        load_planes(help_planes, help_scales, 0)
-        for g in range(GROUPS):
-            load_help(g)
+        load_planes(help_first, help_scales, 0, 0, 1)
+        load_help(0, 1)
+        load_help(1, GROUPS)
+        load_planes(help_later, help_scales, 0, 1, GROUPS)
         load_truth(0)
-        load_planes(truth_planes, truth_scales, TRUTH_PLANE_ROW)
+        load_planes(truth_planes, truth_scales, TRUTH_PLANE_ROW, 0, GROUPS)
         load_truth(1)
         load_truth(2)
         for m in BY_VECTOR:
@@ -210,17 +212,22 @@ def tile_skew_preference_min_s10_kernel(tc, v, help_words, help_scales, truth_wo
         quality_banks = {}
         quality = {}
 
+        def help_columns(bank, m, g, at, width):
+            codes = help_codes[g][:, 2 * at : 2 * (at + width)].bitcast(FP4X4)
+            mx_pass(bank[:, 0:width], m, g, codes, help_planes[g][:, at : at + width], g == 0, False)
+
+        def truth_columns(bank, m, g, at, width):
+            codes = truth_codes[g][:, 4 * at : 4 * (at + width)].bitcast(FP8X4)
+            planes = truth_planes[TRUTH_PLANE_ROW:P, g, at : at + width]
+            mx_pass(bank[:, 0:width], m, g, codes, planes, False, g == GROUPS - 1)
+
         def help_pass(m, n, g):
             if g == 0:
                 quality_banks[(m, n)] = next_bank()
-            codes = help_codes[g][:, n * 1024 : (n + 1) * 1024].bitcast(FP4X4)
-            planes = help_planes[:, g, n * N_TILE : (n + 1) * N_TILE]
-            mx_pass(quality_banks[(m, n)][:], m, g, codes, planes, g == 0, False)
+            help_columns(quality_banks[(m, n)], m, g, n * N_TILE, N_TILE)
 
         def truth_pass(m, n, g):
-            codes = truth_codes[g][:, n * 2048 : (n + 1) * 2048].bitcast(FP8X4)
-            planes = truth_planes[TRUTH_PLANE_ROW:P, g, n * N_TILE : (n + 1) * N_TILE]
-            mx_pass(quality_banks[(m, n)][:], m, g, codes, planes, False, g == GROUPS - 1)
+            truth_columns(quality_banks[(m, n)], m, g, n * N_TILE, N_TILE)
 
         def empty_quality(m, n):
             kept = sbuf([P, N_TILE], F32, "quality%d_%d" % (m, n))
@@ -291,8 +298,6 @@ def tile_skew_preference_min_s10_kernel(tc, v, help_words, help_scales, truth_wo
             empty_quality(m, n)
         interleave_safe(nc.scalar.copy, 2, 1, LAST_SPLIT, N_TILE)
         quantise_safe(2, 1)
-        quality_tile(5, 1)
-        empty_quality(5, 1)
 
         banks = [next_bank() for m in range(SWEEP)]
         for g in every_group:
@@ -301,8 +306,19 @@ def tile_skew_preference_min_s10_kernel(tc, v, help_words, help_scales, truth_wo
         for m in range(SWEEP):
             finish(banks[m], m, 0, 0, N_TILE)
         rest = [(m, 0) for m in range(SWEEP, M_BLOCKS)] + [(m, 1) for m in range(M_BLOCKS)]
-        for m, n in rest:
-            first = 0
-            for width in PIECES.get((m, n), (N_TILE,)):
-                safety_tile(m, n, first, width)
-                first = first + width
+        for m, n in rest[:-2]:
+            safety_tile(m, n, 0, N_TILE)
+        last = M_BLOCKS - 1
+        bank = next_bank()
+        for g in every_group:
+            safe_pass(bank, last, 1, g, 0, N_TILE)
+        quality_banks[(last, 1)] = bank
+        empty_quality(last, 1)
+        safety_tile(last - 1, 1, 0, N_TILE)
+        for first in range(0, N_TILE, P):
+            bank = next_bank()
+            for g in every_group:
+                help_columns(bank, last, g, N_TILE + first, P)
+            for g in every_group:
+                truth_columns(bank, last, g, N_TILE + first, P)
+            finish(bank, last, 1, first, P)

@@ -29,8 +29,8 @@ MOVING_CODES_AT = 64
 STATIONARY_CODES_AT = 192
 STATIONARY_PLANES_AT = 128
 TRUTH_PLANE_ROW = 4
-SWEEP = 2
-LAST_SPLIT = 256
+SWEEP = 5
+SAFE_ORDER = (0, 2, 1)
 
 
 def tile_skew_preference_min_s10_kernel(tc, v, help_words, help_scales, truth_words, truth_scales, safe, out):
@@ -76,8 +76,12 @@ def tile_skew_preference_min_s10_kernel(tc, v, help_words, help_scales, truth_wo
         v_grouped = {m: sbuf([P, K], BF16, "v_grouped%d" % m) for m in BY_VECTOR}
         v_codes = {m: shifted(GROUPS * P, U32, "v_codes%d" % m, STATIONARY_CODES_AT) for m in BY_VECTOR}
         v_planes = {m: shifted(GROUPS * P, U8, "v_planes%d" % m, STATIONARY_PLANES_AT) for m in BY_VECTOR}
-        safe_raw = [sbuf([P, 4, N], BF16, "safe_raw%d" % g) for g in range(GROUPS)]
         halves = [(g, n) for g in range(GROUPS) for n in range(N_TILES)]
+        safe_whole = [sbuf([P, 4, N], BF16, "safe_whole%d" % g) for g in range(GROUPS - 1)]
+        safe_last = [sbuf([P, 4, N_TILE], BF16, "safe_last%d" % n) for n in range(N_TILES)]
+        safe_raw = {(g, n): safe_whole[g][:, :, n * N_TILE : (n + 1) * N_TILE] for g, n in halves[:-N_TILES]}
+        for n in range(N_TILES):
+            safe_raw[(GROUPS - 1, n)] = safe_last[n][:]
         safe_grouped = {h: sbuf([P, N_TILE, 4], BF16, "safe_grouped%d_%d" % h) for h in halves}
         safe_codes = {h: shifted(N_TILE, U32, "safe_codes%d_%d" % h, MOVING_CODES_AT) for h in halves}
         safe_planes = {h: sbuf([P, N_TILE], U8, "safe_planes%d_%d" % h) for h in halves}
@@ -115,10 +119,9 @@ def tile_skew_preference_min_s10_kernel(tc, v, help_words, help_scales, truth_wo
                 out=truth_codes[g].bitcast(I32), in_=truth_words[g].rearrange("p n t -> p (n t)").bitcast(I32)
             )
 
-        def load_safe(g):
-            nc.sync.dma_start(
-                out=safe_raw[g][:], in_=safe[g * K_PASS : (g + 1) * K_PASS, :].rearrange("(p t) n -> p t n", t=4)
-            )
+        def load_safe(raw, g, first, last):
+            rows = safe[g * K_PASS : (g + 1) * K_PASS, first:last]
+            nc.sync.dma_start(out=raw[:], in_=rows.rearrange("(p t) n -> p t n", t=4))
 
         for i in range(len(head_loads)):
             load_head(i)
@@ -126,14 +129,17 @@ def tile_skew_preference_min_s10_kernel(tc, v, help_words, help_scales, truth_wo
         load_help(0, 1)
         load_help(1, GROUPS)
         load_planes(help_later, help_scales, 0, 1, GROUPS)
+        load_quarters(3)
         load_truth(0)
         load_planes(truth_planes, truth_scales, TRUTH_PLANE_ROW, 0, GROUPS)
+        load_safe(safe_whole[0], 0, 0, N)
         load_truth(1)
         load_truth(2)
-        for m in BY_VECTOR:
-            load_quarters(m)
-        for g in range(GROUPS):
-            load_safe(g)
+        load_quarters(4)
+        load_quarters(5)
+        load_safe(safe_whole[1], 1, 0, N)
+        for n in range(N_TILES):
+            load_safe(safe_last[n], 2, n * N_TILE, (n + 1) * N_TILE)
 
         head_words = {}
         for i, load in enumerate(head_loads):
@@ -189,11 +195,10 @@ def tile_skew_preference_min_s10_kernel(tc, v, help_words, help_scales, truth_wo
                 return head_codes[:, at : at + P], head_planes[:, at : at + P]
             return v_codes[m][:, g * P : (g + 1) * P], v_planes[m][:, g * P : (g + 1) * P]
 
-        def interleave_safe(copy, g, n, first, last):
-            at = n * N_TILE
+        def interleave_safe(copy, g, n):
             copy(
-                out=safe_grouped[(g, n)][:, first:last, :].rearrange("p (c i) t -> p c t i", i=4),
-                in_=safe_raw[g][:, :, at + first : at + last].rearrange("p t (c i) -> p c t i", i=4),
+                out=safe_grouped[(g, n)][:].rearrange("p (c i) t -> p c t i", i=4),
+                in_=safe_raw[(g, n)].rearrange("p t (c i) -> p c t i", i=4),
             )
 
         def quantise_safe(g, n):
@@ -210,7 +215,6 @@ def tile_skew_preference_min_s10_kernel(tc, v, help_words, help_scales, truth_wo
             )
 
         quality_banks = {}
-        quality = {}
 
         def help_columns(bank, m, g, at, width):
             codes = help_codes[g][:, 2 * at : 2 * (at + width)].bitcast(FP4X4)
@@ -229,11 +233,6 @@ def tile_skew_preference_min_s10_kernel(tc, v, help_words, help_scales, truth_wo
         def truth_pass(m, n, g):
             truth_columns(quality_banks[(m, n)], m, g, n * N_TILE, N_TILE)
 
-        def empty_quality(m, n):
-            kept = sbuf([P, N_TILE], F32, "quality%d_%d" % (m, n))
-            nc.scalar.copy(out=kept[:], in_=quality_banks[(m, n)][:])
-            quality[(m, n)] = kept
-
         def sweep(one_pass, blocks, groups):
             for g in groups:
                 for m in blocks:
@@ -246,75 +245,77 @@ def tile_skew_preference_min_s10_kernel(tc, v, help_words, help_scales, truth_wo
             for g in range(GROUPS):
                 truth_pass(m, n, g)
 
-        def safe_pass(bank, m, n, g, first, width):
-            cols = slice(first, first + width)
-            codes = safe_codes[(g, n)][:, cols].bitcast(FP8X4)
-            mx_pass(bank[:, 0:width], m, g, codes, safe_planes[(g, n)][:, cols], g == 0, g == GROUPS - 1)
+        def safe_pass(bank, m, n, g):
+            codes = safe_codes[(g, n)].bitcast(FP8X4)
+            mx_pass(bank[:], m, g, codes, safe_planes[(g, n)][:], g == SAFE_ORDER[0], g == SAFE_ORDER[-1])
+
+        def safety_tile(m, n):
+            bank = next_bank()
+            for g in SAFE_ORDER:
+                safe_pass(bank, m, n, g)
+            return bank
+
+        early = {}
+
+        def keep_early(bank, m, n):
+            kept = sbuf([P, N_TILE], F32, "early%d_%d" % (m, n))
+            nc.scalar.activation(out=kept[:], in_=bank[:], func=SIGMOID)
+            early[(m, n)] = kept
+
+        def keep_quality(m, n):
+            keep_early(quality_banks[(m, n)], m, n)
 
         def finish(bank, m, n, first, width):
-            low = quality[(m, n)][:, first : first + width]
-            result = sbuf([P, width], F32, "result%d_%d_%d" % (m, n, first))
-            nc.vector.tensor_tensor(out=low, in0=bank[:, 0:width], in1=low, op=MIN)
-            nc.scalar.activation(out=result[:], in_=low, func=SIGMOID)
+            late = sbuf([P, width], F32, "late%d_%d_%d" % (m, n, first))
+            nc.scalar.activation(out=late[:], in_=bank[:, 0:width], func=SIGMOID)
+            nc.vector.tensor_tensor(out=late[:], in0=late[:], in1=early[(m, n)][:, first : first + width], op=MIN)
             at = n * N_TILE + first
-            nc.sync.dma_start(out=out[m * P : (m + 1) * P, at : at + width], in_=result[:])
-
-        def safety_tile(m, n, first, width):
-            bank = next_bank()
-            for g in range(GROUPS):
-                safe_pass(bank, m, n, g, first, width)
-            finish(bank, m, n, first, width)
+            nc.sync.dma_start(out=out[m * P : (m + 1) * P, at : at + width], in_=late[:])
 
         every_group = range(GROUPS)
+        on_vector = nc.vector.tensor_copy
         for first in range(0, len(units), 2):
             turn_on_tensor(first, min(first + 2, len(units)))
         sweep(help_pass, BY_TENSOR, every_group)
-        sweep(truth_pass, BY_TENSOR, (0,))
-        for m in BY_VECTOR:
-            turn_on_vector(m)
-        for m in BY_TENSOR:
-            for n in range(N_TILES):
-                truth_pass(m, n, 1)
-                truth_pass(m, n, 2)
-                empty_quality(m, n)
-
-        on_vector = nc.vector.tensor_copy
-        interleave_safe(nc.scalar.copy, 0, 1, 0, N_TILE)
-        interleave_safe(on_vector, 0, 0, 0, N_TILE)
+        turn_on_vector(3)
+        sweep(help_pass, (3,), every_group)
+        sweep(truth_pass, (0, 1, 2, 3), (0,))
         for n in range(N_TILES):
-            quality_tile(3, n)
-            empty_quality(3, n)
-        interleave_safe(nc.scalar.copy, 1, 1, 0, N_TILE)
-        interleave_safe(on_vector, 1, 0, 0, N_TILE)
-        quantise_safe(0, 0)
-        quantise_safe(1, 0)
-        interleave_safe(on_vector, 2, 0, 0, N_TILE)
-        quantise_safe(0, 1)
-        quantise_safe(2, 0)
-        interleave_safe(on_vector, 2, 1, 0, LAST_SPLIT)
-        quantise_safe(1, 1)
-        for m, n in ((4, 0), (4, 1), (5, 0)):
+            interleave_safe(on_vector, 0, n)
+        for n in range(N_TILES):
+            quantise_safe(0, n)
+        for blocks in ((0, 1), (2, 3)):
+            sweep(truth_pass, blocks, (1, 2))
+            for m in blocks:
+                for n in range(N_TILES):
+                    keep_quality(m, n)
+        turn_on_vector(4)
+        turn_on_vector(5)
+        quality_tile(4, 0)
+        keep_quality(4, 0)
+        interleave_safe(nc.scalar.copy, 1, 0)
+        for m, n in ((4, 1), (5, 0)):
             quality_tile(m, n)
-            empty_quality(m, n)
-        interleave_safe(nc.scalar.copy, 2, 1, LAST_SPLIT, N_TILE)
+            keep_quality(m, n)
+        interleave_safe(nc.scalar.copy, 2, 1)
+        interleave_safe(on_vector, 2, 0)
+        quantise_safe(2, 0)
+        quantise_safe(1, 0)
+        interleave_safe(on_vector, 1, 1)
+        quantise_safe(1, 1)
         quantise_safe(2, 1)
 
         banks = [next_bank() for m in range(SWEEP)]
-        for g in every_group:
+        for g in SAFE_ORDER:
             for m in range(SWEEP):
-                safe_pass(banks[m], m, 0, g, 0, N_TILE)
+                safe_pass(banks[m], m, 0, g)
         for m in range(SWEEP):
             finish(banks[m], m, 0, 0, N_TILE)
-        rest = [(m, 0) for m in range(SWEEP, M_BLOCKS)] + [(m, 1) for m in range(M_BLOCKS)]
-        for m, n in rest[:-2]:
-            safety_tile(m, n, 0, N_TILE)
         last = M_BLOCKS - 1
-        bank = next_bank()
-        for g in every_group:
-            safe_pass(bank, last, 1, g, 0, N_TILE)
-        quality_banks[(last, 1)] = bank
-        empty_quality(last, 1)
-        safety_tile(last - 1, 1, 0, N_TILE)
+        for m, n in [(m, 0) for m in range(SWEEP, M_BLOCKS)] + [(m, 1) for m in range(last - 1)]:
+            finish(safety_tile(m, n), m, n, 0, N_TILE)
+        keep_early(safety_tile(last, 1), last, 1)
+        finish(safety_tile(last - 1, 1), last - 1, 1, 0, N_TILE)
         for first in range(0, N_TILE, P):
             bank = next_bank()
             for g in every_group:

@@ -30,7 +30,8 @@ STATIONARY_CODES_AT = 192
 STATIONARY_PLANES_AT = 128
 TRUTH_PLANE_ROW = 4
 SWEEP = 5
-SAFE_ORDER = (0, 2, 1)
+SHARED = 256
+SAFE_ORDER = ((0, 1, 2), (0, 2, 1))
 
 
 def tile_skew_preference_min_s10_kernel(tc, v, help_words, help_scales, truth_words, truth_scales, safe, out):
@@ -98,7 +99,8 @@ def tile_skew_preference_min_s10_kernel(tc, v, help_words, help_scales, truth_wo
         def load_quarters(m):
             source = v[m * P : (m + 1) * P, :].rearrange("(j s) (g x) -> j (s g) x", s=4, g=GROUPS)
             for a in (0, 2, 1, 3):
-                nc.sync.dma_start(
+                queue = nc.sync if a < 2 else nc.scalar
+                queue.dma_start(
                     out=v_raw[m][32 * a : 32 * a + 32, :].rearrange("j (b x) -> j b x", x=P),
                     in_=source[:, :, a * P : (a + 1) * P],
                 )
@@ -129,17 +131,10 @@ def tile_skew_preference_min_s10_kernel(tc, v, help_words, help_scales, truth_wo
         load_help(0, 1)
         load_help(1, GROUPS)
         load_planes(help_later, help_scales, 0, 1, GROUPS)
-        load_quarters(3)
         load_truth(0)
         load_planes(truth_planes, truth_scales, TRUTH_PLANE_ROW, 0, GROUPS)
-        load_safe(safe_whole[0], 0, 0, N)
         load_truth(1)
         load_truth(2)
-        load_quarters(4)
-        load_quarters(5)
-        load_safe(safe_whole[1], 1, 0, N)
-        for n in range(N_TILES):
-            load_safe(safe_last[n], 2, n * N_TILE, (n + 1) * N_TILE)
 
         head_words = {}
         for i, load in enumerate(head_loads):
@@ -195,10 +190,10 @@ def tile_skew_preference_min_s10_kernel(tc, v, help_words, help_scales, truth_wo
                 return head_codes[:, at : at + P], head_planes[:, at : at + P]
             return v_codes[m][:, g * P : (g + 1) * P], v_planes[m][:, g * P : (g + 1) * P]
 
-        def interleave_safe(copy, g, n):
+        def interleave_safe(copy, g, n, first, last):
             copy(
-                out=safe_grouped[(g, n)][:].rearrange("p (c i) t -> p c t i", i=4),
-                in_=safe_raw[(g, n)].rearrange("p t (c i) -> p c t i", i=4),
+                out=safe_grouped[(g, n)][:, first:last, :].rearrange("p (c i) t -> p c t i", i=4),
+                in_=safe_raw[(g, n)][:, :, first:last].rearrange("p t (c i) -> p c t i", i=4),
             )
 
         def quantise_safe(g, n):
@@ -247,11 +242,11 @@ def tile_skew_preference_min_s10_kernel(tc, v, help_words, help_scales, truth_wo
 
         def safe_pass(bank, m, n, g):
             codes = safe_codes[(g, n)].bitcast(FP8X4)
-            mx_pass(bank[:], m, g, codes, safe_planes[(g, n)][:], g == SAFE_ORDER[0], g == SAFE_ORDER[-1])
+            mx_pass(bank[:], m, g, codes, safe_planes[(g, n)][:], g == SAFE_ORDER[n][0], g == SAFE_ORDER[n][-1])
 
         def safety_tile(m, n):
             bank = next_bank()
-            for g in SAFE_ORDER:
+            for g in SAFE_ORDER[n]:
                 safe_pass(bank, m, n, g)
             return bank
 
@@ -276,37 +271,45 @@ def tile_skew_preference_min_s10_kernel(tc, v, help_words, help_scales, truth_wo
         on_vector = nc.vector.tensor_copy
         for first in range(0, len(units), 2):
             turn_on_tensor(first, min(first + 2, len(units)))
+        for m in BY_VECTOR:
+            load_quarters(m)
+        for g in range(GROUPS - 1):
+            load_safe(safe_whole[g], g, 0, N)
+        for n in range(N_TILES):
+            load_safe(safe_last[n], GROUPS - 1, n * N_TILE, (n + 1) * N_TILE)
+
         sweep(help_pass, BY_TENSOR, every_group)
-        turn_on_vector(3)
-        sweep(help_pass, (3,), every_group)
-        sweep(truth_pass, (0, 1, 2, 3), (0,))
+        sweep(truth_pass, BY_TENSOR, (0,))
+        for m in BY_VECTOR:
+            turn_on_vector(m)
+        for m in BY_TENSOR:
+            for n in range(N_TILES):
+                truth_pass(m, n, 1)
+                truth_pass(m, n, 2)
+                keep_quality(m, n)
         for n in range(N_TILES):
-            interleave_safe(on_vector, 0, n)
+            quality_tile(3, n)
+            keep_quality(3, n)
+        interleave_safe(nc.scalar.copy, 0, 1, 0, N_TILE)
+        interleave_safe(on_vector, 0, 0, 0, N_TILE)
         for n in range(N_TILES):
-            quantise_safe(0, n)
-        for blocks in ((0, 1), (2, 3)):
-            sweep(truth_pass, blocks, (1, 2))
-            for m in blocks:
-                for n in range(N_TILES):
-                    keep_quality(m, n)
-        turn_on_vector(4)
-        turn_on_vector(5)
-        quality_tile(4, 0)
-        keep_quality(4, 0)
-        interleave_safe(nc.scalar.copy, 1, 0)
-        for m, n in ((4, 1), (5, 0)):
-            quality_tile(m, n)
-            keep_quality(m, n)
-        interleave_safe(nc.scalar.copy, 2, 1)
-        interleave_safe(on_vector, 2, 0)
-        quantise_safe(2, 0)
+            quality_tile(4, n)
+            keep_quality(4, n)
+        quantise_safe(0, 0)
+        interleave_safe(on_vector, 1, 0, 0, N_TILE)
+        interleave_safe(nc.scalar.copy, 2, 0, SHARED, N_TILE)
+        interleave_safe(on_vector, 2, 0, 0, SHARED)
         quantise_safe(1, 0)
-        interleave_safe(on_vector, 1, 1)
-        quantise_safe(1, 1)
-        quantise_safe(2, 1)
+        quantise_safe(2, 0)
+        quality_tile(5, 0)
+        keep_quality(5, 0)
+        interleave_safe(nc.scalar.copy, 1, 1, 0, N_TILE)
+        interleave_safe(on_vector, 2, 1, 0, N_TILE)
+        for g in (0, 2, 1):
+            quantise_safe(g, 1)
 
         banks = [next_bank() for m in range(SWEEP)]
-        for g in SAFE_ORDER:
+        for g in SAFE_ORDER[0]:
             for m in range(SWEEP):
                 safe_pass(banks[m], m, 0, g)
         for m in range(SWEEP):

@@ -65,9 +65,10 @@ def tile_skew_preference_min_s10_kernel(tc, v, help_words, help_scales, truth_wo
         help_all = shifted(GROUPS * 2 * N, U8, "help_all", MOVING_CODES_AT)
         help_codes = [help_all[:, g * 2 * N : (g + 1) * 2 * N] for g in range(GROUPS)]
         truth_codes = [shifted(4 * N, U8, "truth_codes%d" % g, MOVING_CODES_AT) for g in range(GROUPS)]
-        units = [(m, g) for m in BY_TENSOR for g in range(GROUPS)]
-        head_loads = [units[0:1], units[1:GROUPS]] + [units[m * GROUPS : (m + 1) * GROUPS] for m in BY_TENSOR[1:]]
+        head_loads = [[(0, 0)], [(1, 0)], [(0, 1), (0, 2)], [(1, 1), (1, 2)], [(2, 0), (2, 1), (2, 2)]]
+        units = [unit for load in head_loads for unit in load]
         head_raw = [sbuf([P, len(load) * K_PASS], BF16, "head_raw%d" % i) for i, load in enumerate(head_loads)]
+        late_sorted = sbuf([P, GROUPS * 256], F32, "late_sorted")
         head_grouped = sbuf([P, len(units) * K_PASS], BF16, "head_grouped")
         head_codes = shifted(len(units) * P, U32, "head_codes", STATIONARY_CODES_AT)
         head_planes = shifted(len(units) * P, U8, "head_planes", STATIONARY_PLANES_AT)
@@ -116,6 +117,10 @@ def tile_skew_preference_min_s10_kernel(tc, v, help_words, help_scales, truth_wo
                 in_=help_words[first:last].rearrange("g p b -> p g b").bitcast(I32),
             )
 
+        def load_first_help(n):
+            cols = slice(n * 2 * N_TILE, (n + 1) * 2 * N_TILE)
+            nc.sync.dma_start(out=help_codes[0][:, cols].bitcast(I32), in_=help_words[0][:, cols].bitcast(I32))
+
         def load_truth(g):
             nc.sync.dma_start(
                 out=truth_codes[g].bitcast(I32), in_=truth_words[g].rearrange("p n t -> p (n t)").bitcast(I32)
@@ -125,29 +130,45 @@ def tile_skew_preference_min_s10_kernel(tc, v, help_words, help_scales, truth_wo
             rows = safe[g * K_PASS : (g + 1) * K_PASS, first:last]
             nc.sync.dma_start(out=raw[:], in_=rows.rearrange("(p t) n -> p t n", t=4))
 
-        for i in range(len(head_loads)):
+        for i in range(len(head_loads) - 1):
             load_head(i)
         load_planes(help_first, help_scales, 0, 0, 1)
-        load_help(0, 1)
-        load_help(1, GROUPS)
+        for n in range(N_TILES):
+            load_first_help(n)
+        load_head(len(head_loads) - 1)
+        load_help(1, 2)
         load_planes(help_later, help_scales, 0, 1, GROUPS)
+        load_help(2, 3)
         load_truth(0)
         load_planes(truth_planes, truth_scales, TRUTH_PLANE_ROW, 0, GROUPS)
         load_truth(1)
         load_truth(2)
 
         head_words = {}
-        for i, load in enumerate(head_loads):
+        for i, load in enumerate(head_loads[:-1]):
             for q, unit in enumerate(load):
-                head_words[unit] = head_raw[i][:].bitcast(F32)[:, 256 * q : 256 * (q + 1)]
+                words = head_raw[i][:].bitcast(F32)
+                head_words[unit] = [words[:, 256 * q + u : 256 * (q + 1) : 2] for u in range(2)]
+        for q, unit in enumerate(head_loads[-1]):
+            head_words[unit] = [late_sorted[:, 256 * q + u * P : 256 * q + (u + 1) * P] for u in range(2)]
+
+        def sort_late(first, last):
+            cols = slice(256 * first, 256 * last)
+            nc.vector.tensor_copy(
+                out=late_sorted[:, cols].rearrange("p (q u i) -> p q u i", u=2, i=P),
+                in_=head_raw[-1][:].bitcast(F32)[:, cols].rearrange("p (q i u) -> p q u i", u=2, i=P),
+            )
 
         def turn_on_tensor(first, last):
             bank = next_bank()
-            count = last - first
             for q, unit in enumerate(units[first:last]):
                 for u in range(2):
                     at = (2 * q + u) * P
-                    nc.tensor.transpose(bank[:, at : at + P], head_words[unit][:, u:256:2], identity[:])
+                    nc.tensor.transpose(bank[:, at : at + P], head_words[unit][u], identity[:])
+            return bank
+
+        def quantise_head(bank, first, last):
+            count = last - first
             grouped = head_grouped[:, first * K_PASS : last * K_PASS]
             nc.scalar.copy(
                 out=grouped.bitcast(F32).rearrange("p (q r u) -> p q r u", q=count, u=2),
@@ -269,8 +290,15 @@ def tile_skew_preference_min_s10_kernel(tc, v, help_words, help_scales, truth_wo
 
         every_group = range(GROUPS)
         on_vector = nc.vector.tensor_copy
-        for first in range(0, len(units), 2):
-            turn_on_tensor(first, min(first + 2, len(units)))
+        for first in (0, 2, 4):
+            quantise_head(turn_on_tensor(first, first + 2), first, first + 2)
+        for n in range(N_TILES):
+            for m in (0, 1):
+                help_pass(m, n, 0)
+        sort_late(0, 2)
+        sort_late(2, 3)
+        for first, last in ((6, 8), (8, 9)):
+            quantise_head(turn_on_tensor(first, last), first, last)
         for m in BY_VECTOR:
             load_quarters(m)
         for g in range(GROUPS - 1):
@@ -278,7 +306,9 @@ def tile_skew_preference_min_s10_kernel(tc, v, help_words, help_scales, truth_wo
         for n in range(N_TILES):
             load_safe(safe_last[n], GROUPS - 1, n * N_TILE, (n + 1) * N_TILE)
 
-        sweep(help_pass, BY_TENSOR, every_group)
+        sweep(help_pass, (0, 1), (1,))
+        sweep(help_pass, (2,), (0, 1))
+        sweep(help_pass, BY_TENSOR, (2,))
         sweep(truth_pass, BY_TENSOR, (0,))
         for m in BY_VECTOR:
             turn_on_vector(m)

@@ -18,13 +18,14 @@ MIN = mybir.AluOpType.min
 
 P = 128
 K_PASS = 512
+WORDS = K_PASS // 2
 GROUPS = K // K_PASS
-M_BLOCKS = M // P
+M_TILES = M // P
 N_TILE = 512
 N_TILES = N // N_TILE
 BANKS = 8
-BY_TENSOR = (0, 1, 2)
-BY_VECTOR = (3, 4, 5)
+BY_TENSOR = (0, 1, 2, 3)
+BY_VECTOR = (4, 5)
 MOVING_CODES_AT = 64
 STATIONARY_CODES_AT = 192
 STATIONARY_PLANES_AT = 128
@@ -50,25 +51,27 @@ def tile_skew_preference_min_s10_kernel(tc, v, help_words, help_scales, truth_wo
             tile = sbuf([P, at // size + width], dtype, name)
             return tile[:, at // size :]
 
-        taken = []
+        free_banks = list(range(BANKS))
 
-        def next_bank():
-            bank = psum.tile([P, N_TILE], F32, name="bank%d" % (len(taken) % BANKS))
-            taken.append(bank)
-            return bank
+        def take_bank():
+            number = free_banks.pop(0)
+            tile = psum.tile([P, N_TILE], F32, name="bank%d" % number)
+            return number, tile
 
         identity = sbuf([P, P], F32, "identity")
         help_first = sbuf([P, 1, N], U8, "help_first")
         help_later = sbuf([P, GROUPS - 1, N], U8, "help_later")
         help_planes = [help_first[:, 0, :]] + [help_later[:, g, :] for g in range(GROUPS - 1)]
         truth_planes = sbuf([P, GROUPS, N], U8, "truth_planes")
-        help_all = shifted(GROUPS * 2 * N, U8, "help_all", MOVING_CODES_AT)
-        help_codes = [help_all[:, g * 2 * N : (g + 1) * 2 * N] for g in range(GROUPS)]
+        help_codes = [shifted(2 * N, U8, "help_codes%d" % g, MOVING_CODES_AT) for g in range(GROUPS)]
         truth_codes = [shifted(4 * N, U8, "truth_codes%d" % g, MOVING_CODES_AT) for g in range(GROUPS)]
-        head_loads = [[(0, 0)], [(1, 0)], [(0, 1), (0, 2)], [(1, 1), (1, 2)], [(2, 0), (2, 1), (2, 2)]]
-        units = [unit for load in head_loads for unit in load]
-        head_raw = [sbuf([P, len(load) * K_PASS], BF16, "head_raw%d" % i) for i, load in enumerate(head_loads)]
-        late_sorted = sbuf([P, GROUPS * 256], F32, "late_sorted")
+        early_loads = [[(0, 0)], [(1, 0), (2, 0)]]
+        late_loads = [[(m, 1), (m, 2)] for m in range(3)] + [[(3, 0), (3, 1), (3, 2)]]
+        units = [unit for load in early_loads + late_loads for unit in load]
+        early_count = sum(len(load) for load in early_loads)
+        early_raw = [sbuf([P, len(load) * K_PASS], BF16, "early_raw%d" % i) for i, load in enumerate(early_loads)]
+        late_raw = [sbuf([P, len(load) * K_PASS], BF16, "late_raw%d" % i) for i, load in enumerate(late_loads)]
+        late_sorted = [sbuf([P, len(load) * WORDS], F32, "late_sorted%d" % i) for i, load in enumerate(late_loads)]
         head_grouped = sbuf([P, len(units) * K_PASS], BF16, "head_grouped")
         head_codes = shifted(len(units) * P, U32, "head_codes", STATIONARY_CODES_AT)
         head_planes = shifted(len(units) * P, U8, "head_planes", STATIONARY_PLANES_AT)
@@ -92,10 +95,13 @@ def tile_skew_preference_min_s10_kernel(tc, v, help_words, help_scales, truth_wo
             nc.vector.memset(planes[:].rearrange("p g n -> p (g n)").bitcast(I32), 0)
         make_identity(nc, identity[:])
 
-        def load_head(i):
-            m, first = head_loads[i][0]
-            last = first + len(head_loads[i])
-            nc.sync.dma_start(out=head_raw[i][:], in_=v[m * P : (m + 1) * P, first * K_PASS : last * K_PASS])
+        def load_units(raw, load):
+            (m, g), (last_m, last_g) = load[0], load[-1]
+            rows = v[m * P : (last_m + 1) * P, g * K_PASS : (last_g + 1) * K_PASS]
+            tiles = last_m + 1 - m
+            nc.sync.dma_start(
+                out=raw[:].rearrange("p (m x) -> p m x", m=tiles), in_=rows.rearrange("(m p) x -> p m x", p=P)
+            )
 
         def load_quarters(m):
             source = v[m * P : (m + 1) * P, :].rearrange("(j s) (g x) -> j (s g) x", s=4, g=GROUPS)
@@ -111,15 +117,8 @@ def tile_skew_preference_min_s10_kernel(tc, v, help_words, help_scales, truth_wo
             for r in range(4):
                 nc.sync.dma_start(out=planes[row + r : P : 32, :, :].bitcast(I32), in_=by_row[r])
 
-        def load_help(first, last):
-            nc.sync.dma_start(
-                out=help_all[:, first * 2 * N : last * 2 * N].bitcast(I32).rearrange("p (g b) -> p g b", g=last - first),
-                in_=help_words[first:last].rearrange("g p b -> p g b").bitcast(I32),
-            )
-
-        def load_first_help(n):
-            cols = slice(n * 2 * N_TILE, (n + 1) * 2 * N_TILE)
-            nc.sync.dma_start(out=help_codes[0][:, cols].bitcast(I32), in_=help_words[0][:, cols].bitcast(I32))
+        def load_help(g):
+            nc.sync.dma_start(out=help_codes[g].bitcast(I32), in_=help_words[g].bitcast(I32))
 
         def load_truth(g):
             nc.sync.dma_start(
@@ -130,67 +129,71 @@ def tile_skew_preference_min_s10_kernel(tc, v, help_words, help_scales, truth_wo
             rows = safe[g * K_PASS : (g + 1) * K_PASS, first:last]
             nc.sync.dma_start(out=raw[:], in_=rows.rearrange("(p t) n -> p t n", t=4))
 
-        for i in range(len(head_loads) - 1):
-            load_head(i)
+        for raw, load in zip(early_raw, early_loads):
+            load_units(raw, load)
+        load_help(0)
         load_planes(help_first, help_scales, 0, 0, 1)
-        for n in range(N_TILES):
-            load_first_help(n)
-        load_head(len(head_loads) - 1)
-        load_help(1, 2)
+        for raw, load in zip(late_raw[:-1], late_loads[:-1]):
+            load_units(raw, load)
+        load_help(1)
         load_planes(help_later, help_scales, 0, 1, GROUPS)
-        load_help(2, 3)
+        load_help(2)
         load_truth(0)
         load_planes(truth_planes, truth_scales, TRUTH_PLANE_ROW, 0, GROUPS)
+        load_units(late_raw[-1], late_loads[-1])
         load_truth(1)
         load_truth(2)
 
         head_words = {}
-        for i, load in enumerate(head_loads[:-1]):
+        for raw, load in zip(early_raw, early_loads):
             for q, unit in enumerate(load):
-                words = head_raw[i][:].bitcast(F32)
-                head_words[unit] = [words[:, 256 * q + u : 256 * (q + 1) : 2] for u in range(2)]
-        for q, unit in enumerate(head_loads[-1]):
-            head_words[unit] = [late_sorted[:, 256 * q + u * P : 256 * q + (u + 1) * P] for u in range(2)]
+                words = raw[:].bitcast(F32)
+                head_words[unit] = [words[:, WORDS * q + u : WORDS * (q + 1) : 2] for u in range(2)]
+        for tile, load in zip(late_sorted, late_loads):
+            for q, unit in enumerate(load):
+                head_words[unit] = [tile[:, WORDS * q + u * P : WORDS * q + (u + 1) * P] for u in range(2)]
 
-        def sort_late(first, last):
-            cols = slice(256 * first, 256 * last)
+        def sort_late(i, first, last):
+            cols = slice(WORDS * first, WORDS * last)
             nc.vector.tensor_copy(
-                out=late_sorted[:, cols].rearrange("p (q u i) -> p q u i", u=2, i=P),
-                in_=head_raw[-1][:].bitcast(F32)[:, cols].rearrange("p (q i u) -> p q u i", u=2, i=P),
+                out=late_sorted[i][:, cols].rearrange("p (q u i) -> p q u i", u=2, i=P),
+                in_=late_raw[i][:].bitcast(F32)[:, cols].rearrange("p (q i u) -> p q u i", u=2, i=P),
             )
 
         def turn_on_tensor(first, last):
-            bank = next_bank()
+            number, bank = take_bank()
             for q, unit in enumerate(units[first:last]):
                 for u in range(2):
                     at = (2 * q + u) * P
                     nc.tensor.transpose(bank[:, at : at + P], head_words[unit][u], identity[:])
-            return bank
+            return number, bank, first, last
 
-        def quantise_head(bank, first, last):
+        def quantise_head(number, bank, first, last):
             count = last - first
             grouped = head_grouped[:, first * K_PASS : last * K_PASS]
             nc.scalar.copy(
                 out=grouped.bitcast(F32).rearrange("p (q r u) -> p q r u", q=count, u=2),
-                in_=bank[:, 0 : count * 256].rearrange("p (q u r) -> p q r u", q=count, u=2),
+                in_=bank[:, 0 : count * WORDS].rearrange("p (q u r) -> p q r u", q=count, u=2),
             )
+            free_banks.append(number)
             nc.vector.quantize_mx(
                 out=head_codes[:, first * P : last * P].bitcast(FP8X4), scales=head_planes[:, first * P : last * P], in_=grouped
             )
 
         def sort_words(m, g):
             nc.vector.tensor_copy(
-                out=v_sorted[m][:, 256 * g : 256 * (g + 1)].rearrange("p (s u i) -> p s u i", s=4, u=2),
+                out=v_sorted[m][:, WORDS * g : WORDS * (g + 1)].rearrange("p (s u i) -> p s u i", s=4, u=2),
                 in_=v_raw[m][:].bitcast(F32).rearrange("p (s g i u) -> p g s u i", s=4, g=GROUPS, u=2)[:, g],
             )
 
         def turn_squares(m, g):
-            nc.vector.transpose(out=v_turned[m][:, 256 * g : 256 * (g + 1)], in_=v_sorted[m][:, 256 * g : 256 * (g + 1)])
+            cols = slice(WORDS * g, WORDS * (g + 1))
+            nc.vector.transpose(out=v_turned[m][:, cols], in_=v_sorted[m][:, cols])
 
         def pair_words(m, g):
             nc.vector.tensor_copy(
                 out=v_grouped[m][:, g * K_PASS : (g + 1) * K_PASS].bitcast(F32).rearrange("p (j h w) -> p h j w", h=2, w=4),
-                in_=v_turned[m][:, 256 * g : 256 * (g + 1)].rearrange("p (h w j) -> p h j w", h=2, w=4),
+                in_=v_turned[m][:, WORDS * g : WORDS * (g + 1)].rearrange("p (h w j) -> p h j w", h=2, w=4),
             )
 
         def quantise_v(m, g):
@@ -243,17 +246,17 @@ def tile_skew_preference_min_s10_kernel(tc, v, help_words, help_scales, truth_wo
 
         def help_pass(m, n, g):
             if g == 0:
-                quality_banks[(m, n)] = next_bank()
-            help_columns(quality_banks[(m, n)], m, g, n * N_TILE, N_TILE)
+                quality_banks[(m, n)] = take_bank()
+            help_columns(quality_banks[(m, n)][1], m, g, n * N_TILE, N_TILE)
 
         def truth_pass(m, n, g):
-            truth_columns(quality_banks[(m, n)], m, g, n * N_TILE, N_TILE)
+            truth_columns(quality_banks[(m, n)][1], m, g, n * N_TILE, N_TILE)
 
-        def sweep(one_pass, blocks, groups):
+        def help_sweep(tiles, groups):
             for g in groups:
-                for m in blocks:
+                for m in tiles:
                     for n in range(N_TILES):
-                        one_pass(m, n, g)
+                        help_pass(m, n, g)
 
         def quality_tile(m, n):
             for g in range(GROUPS):
@@ -266,39 +269,42 @@ def tile_skew_preference_min_s10_kernel(tc, v, help_words, help_scales, truth_wo
             mx_pass(bank[:], m, g, codes, safe_planes[(g, n)][:], g == SAFE_ORDER[n][0], g == SAFE_ORDER[n][-1])
 
         def safety_tile(m, n):
-            bank = next_bank()
+            number, bank = take_bank()
             for g in SAFE_ORDER[n]:
                 safe_pass(bank, m, n, g)
-            return bank
+            return number, bank
 
         early = {}
 
-        def keep_early(bank, m, n):
+        def keep_early(number, bank, m, n):
             kept = sbuf([P, N_TILE], F32, "early%d_%d" % (m, n))
             nc.scalar.activation(out=kept[:], in_=bank[:], func=SIGMOID)
+            free_banks.append(number)
             early[(m, n)] = kept
 
         def keep_quality(m, n):
-            keep_early(quality_banks[(m, n)], m, n)
+            keep_early(*quality_banks[(m, n)], m, n)
 
-        def finish(bank, m, n, first, width):
+        def finish(number, bank, m, n, first, width):
             late = sbuf([P, width], F32, "late%d_%d_%d" % (m, n, first))
             nc.scalar.activation(out=late[:], in_=bank[:, 0:width], func=SIGMOID)
+            free_banks.append(number)
             nc.vector.tensor_tensor(out=late[:], in0=late[:], in1=early[(m, n)][:, first : first + width], op=MIN)
             at = n * N_TILE + first
             nc.sync.dma_start(out=out[m * P : (m + 1) * P, at : at + width], in_=late[:])
 
         every_group = range(GROUPS)
         on_vector = nc.vector.tensor_copy
-        for first in (0, 2, 4):
-            quantise_head(turn_on_tensor(first, first + 2), first, first + 2)
-        for n in range(N_TILES):
-            for m in (0, 1):
-                help_pass(m, n, 0)
-        sort_late(0, 2)
-        sort_late(2, 3)
-        for first, last in ((6, 8), (8, 9)):
-            quantise_head(turn_on_tensor(first, last), first, last)
+        for first in range(early_count):
+            quantise_head(*turn_on_tensor(first, first + 1))
+        help_sweep((0, 1), (0,))
+        for i in range(3):
+            sort_late(i, 0, 2)
+        turned = [turn_on_tensor(first, first + 2) for first in range(early_count, early_count + 6, 2)]
+        for bank in turned:
+            quantise_head(*bank)
+        sort_late(3, 0, 2)
+        sort_late(3, 2, 3)
         for m in BY_VECTOR:
             load_quarters(m)
         for g in range(GROUPS - 1):
@@ -306,13 +312,17 @@ def tile_skew_preference_min_s10_kernel(tc, v, help_words, help_scales, truth_wo
         for n in range(N_TILES):
             load_safe(safe_last[n], GROUPS - 1, n * N_TILE, (n + 1) * N_TILE)
 
-        sweep(help_pass, (0, 1), (1,))
-        sweep(help_pass, (2,), (0, 1))
-        sweep(help_pass, BY_TENSOR, (2,))
-        sweep(truth_pass, BY_TENSOR, (0,))
+        help_sweep((2,), (0,))
+        help_sweep(range(3), (1, 2))
+        for m in range(3):
+            for n in range(N_TILES):
+                truth_pass(m, n, 0)
+        turned = [turn_on_tensor(first, min(first + 2, len(units))) for first in range(early_count + 6, len(units), 2)]
+        for bank in turned:
+            quantise_head(*bank)
         for m in BY_VECTOR:
             turn_on_vector(m)
-        for m in BY_TENSOR:
+        for m in range(3):
             for n in range(N_TILES):
                 truth_pass(m, n, 1)
                 truth_pass(m, n, 2)
@@ -338,21 +348,21 @@ def tile_skew_preference_min_s10_kernel(tc, v, help_words, help_scales, truth_wo
         for g in (0, 2, 1):
             quantise_safe(g, 1)
 
-        banks = [next_bank() for m in range(SWEEP)]
+        banks = [take_bank() for m in range(SWEEP)]
         for g in SAFE_ORDER[0]:
             for m in range(SWEEP):
-                safe_pass(banks[m], m, 0, g)
+                safe_pass(banks[m][1], m, 0, g)
         for m in range(SWEEP):
-            finish(banks[m], m, 0, 0, N_TILE)
-        last = M_BLOCKS - 1
-        for m, n in [(m, 0) for m in range(SWEEP, M_BLOCKS)] + [(m, 1) for m in range(last - 1)]:
-            finish(safety_tile(m, n), m, n, 0, N_TILE)
-        keep_early(safety_tile(last, 1), last, 1)
-        finish(safety_tile(last - 1, 1), last - 1, 1, 0, N_TILE)
+            finish(*banks[m], m, 0, 0, N_TILE)
+        last = M_TILES - 1
+        for m, n in [(m, 0) for m in range(SWEEP, M_TILES)] + [(m, 1) for m in range(last - 1)]:
+            finish(*safety_tile(m, n), m, n, 0, N_TILE)
+        keep_early(*safety_tile(last, 1), last, 1)
+        finish(*safety_tile(last - 1, 1), last - 1, 1, 0, N_TILE)
         for first in range(0, N_TILE, P):
-            bank = next_bank()
+            number, bank = take_bank()
             for g in every_group:
                 help_columns(bank, last, g, N_TILE + first, P)
             for g in every_group:
                 truth_columns(bank, last, g, N_TILE + first, P)
-            finish(bank, last, 1, first, P)
+            finish(number, bank, last, 1, first, P)

@@ -24,8 +24,8 @@ M_TILES = M // P
 N_TILE = 512
 N_TILES = N // N_TILE
 BANKS = 8
-BY_TENSOR = (0, 1, 2, 3)
-BY_VECTOR = (4, 5)
+BY_TENSOR = (0, 1, 2)
+BY_VECTOR = (3, 4, 5)
 MOVING_CODES_AT = 64
 STATIONARY_CODES_AT = 192
 STATIONARY_PLANES_AT = 128
@@ -66,7 +66,7 @@ def tile_skew_preference_min_s10_kernel(tc, v, help_words, help_scales, truth_wo
         help_codes = [shifted(2 * N, U8, "help_codes%d" % g, MOVING_CODES_AT) for g in range(GROUPS)]
         truth_codes = [shifted(4 * N, U8, "truth_codes%d" % g, MOVING_CODES_AT) for g in range(GROUPS)]
         early_loads = [[(0, 0)], [(1, 0), (2, 0)]]
-        late_loads = [[(m, 1), (m, 2)] for m in range(3)] + [[(3, 0), (3, 1), (3, 2)]]
+        late_loads = [[(m, 1), (m, 2)] for m in BY_TENSOR]
         units = [unit for load in early_loads + late_loads for unit in load]
         early_count = sum(len(load) for load in early_loads)
         early_raw = [sbuf([P, len(load) * K_PASS], BF16, "early_raw%d" % i) for i, load in enumerate(early_loads)]
@@ -133,14 +133,13 @@ def tile_skew_preference_min_s10_kernel(tc, v, help_words, help_scales, truth_wo
             load_units(raw, load)
         load_help(0)
         load_planes(help_first, help_scales, 0, 0, 1)
-        for raw, load in zip(late_raw[:-1], late_loads[:-1]):
+        for raw, load in zip(late_raw, late_loads):
             load_units(raw, load)
         load_help(1)
         load_planes(help_later, help_scales, 0, 1, GROUPS)
         load_help(2)
         load_truth(0)
         load_planes(truth_planes, truth_scales, TRUTH_PLANE_ROW, 0, GROUPS)
-        load_units(late_raw[-1], late_loads[-1])
         load_truth(1)
         load_truth(2)
 
@@ -153,11 +152,10 @@ def tile_skew_preference_min_s10_kernel(tc, v, help_words, help_scales, truth_wo
             for q, unit in enumerate(load):
                 head_words[unit] = [tile[:, WORDS * q + u * P : WORDS * q + (u + 1) * P] for u in range(2)]
 
-        def sort_late(i, first, last):
-            cols = slice(WORDS * first, WORDS * last)
+        def sort_late(i):
             nc.vector.tensor_copy(
-                out=late_sorted[i][:, cols].rearrange("p (q u i) -> p q u i", u=2, i=P),
-                in_=late_raw[i][:].bitcast(F32)[:, cols].rearrange("p (q i u) -> p q u i", u=2, i=P),
+                out=late_sorted[i][:].rearrange("p (q u i) -> p q u i", u=2, i=P),
+                in_=late_raw[i][:].bitcast(F32).rearrange("p (q i u) -> p q u i", u=2, i=P),
             )
 
         def turn_on_tensor(first, last):
@@ -298,13 +296,11 @@ def tile_skew_preference_min_s10_kernel(tc, v, help_words, help_scales, truth_wo
         for first in range(early_count):
             quantise_head(*turn_on_tensor(first, first + 1))
         help_sweep((0, 1), (0,))
-        for i in range(3):
-            sort_late(i, 0, 2)
-        turned = [turn_on_tensor(first, first + 2) for first in range(early_count, early_count + 6, 2)]
+        for i in range(len(late_loads)):
+            sort_late(i)
+        turned = [turn_on_tensor(first, first + 2) for first in range(early_count, len(units), 2)]
         for bank in turned:
             quantise_head(*bank)
-        sort_late(3, 0, 2)
-        sort_late(3, 2, 3)
         for m in BY_VECTOR:
             load_quarters(m)
         for g in range(GROUPS - 1):
@@ -313,22 +309,21 @@ def tile_skew_preference_min_s10_kernel(tc, v, help_words, help_scales, truth_wo
             load_safe(safe_last[n], GROUPS - 1, n * N_TILE, (n + 1) * N_TILE)
 
         help_sweep((2,), (0,))
-        help_sweep(range(3), (1, 2))
-        for m in range(3):
+        help_sweep(BY_TENSOR, (1, 2))
+        for m in BY_TENSOR:
             for n in range(N_TILES):
                 truth_pass(m, n, 0)
-        turned = [turn_on_tensor(first, min(first + 2, len(units))) for first in range(early_count + 6, len(units), 2)]
-        for bank in turned:
-            quantise_head(*bank)
         for m in BY_VECTOR:
             turn_on_vector(m)
-        for m in range(3):
+        for m in BY_TENSOR:
             for n in range(N_TILES):
                 truth_pass(m, n, 1)
                 truth_pass(m, n, 2)
                 keep_quality(m, n)
+        help_sweep((3,), every_group)
         for n in range(N_TILES):
-            quality_tile(3, n)
+            for g in every_group:
+                truth_pass(3, n, g)
             keep_quality(3, n)
         interleave_safe(nc.scalar.copy, 0, 1, 0, N_TILE)
         interleave_safe(on_vector, 0, 0, 0, N_TILE)

@@ -32,6 +32,9 @@ STATIONARY_PLANES_AT = 128
 TRUTH_PLANE_ROW = 4
 SWEEP = 5
 SHARED = 256
+WARM_WIDTH = 256
+WARM_BEFORE = 4
+WARM_AFTER = 2
 SAFE_ORDER = ((0, 1, 2), (0, 2, 1))
 
 
@@ -91,8 +94,18 @@ def tile_skew_preference_min_s10_kernel(tc, v, help_words, help_scales, truth_wo
         safe_codes = {h: shifted(N_TILE, U32, "safe_codes%d_%d" % h, MOVING_CODES_AT) for h in halves}
         safe_planes = {h: sbuf([P, N_TILE], U8, "safe_planes%d_%d" % h) for h in halves}
 
-        for planes in (help_first, help_later, truth_planes):
+        zeros = sbuf([P, 4 * WARM_WIDTH], BF16, "zeros")
+        zero_codes = sbuf([P, WARM_WIDTH], U32, "zero_codes")
+        zero_planes = sbuf([P, WARM_WIDTH], U8, "zero_planes")
+
+        def clear(planes):
             nc.vector.memset(planes[:].rearrange("p g n -> p (g n)").bitcast(I32), 0)
+
+        nc.vector.memset(zeros[:].bitcast(I32), 0)
+        clear(help_first)
+        nc.vector.quantize_mx(out=zero_codes[:].bitcast(FP8X4), scales=zero_planes[:], in_=zeros[:])
+        clear(help_later)
+        clear(truth_planes)
         make_identity(nc, identity[:])
 
         def load_units(raw, load):
@@ -293,8 +306,26 @@ def tile_skew_preference_min_s10_kernel(tc, v, help_words, help_scales, truth_wo
 
         every_group = range(GROUPS)
         on_vector = nc.vector.tensor_copy
+
+
+        def warm_up(count):
+            number, bank = take_bank()
+            for i in range(count):
+                nc.tensor.matmul_mx(
+                    out=bank[:, 0:WARM_WIDTH],
+                    lhsT=zero_codes[:, 0:P].bitcast(FP8X4),
+                    lhsT_scale=zero_planes[:, 0:P],
+                    rhs=zero_codes[:].bitcast(FP8X4),
+                    rhs_scale=zero_planes[:],
+                    start=True,
+                    stop=True,
+                )
+            free_banks.append(number)
+
+        warm_up(WARM_BEFORE)
         for first in range(early_count):
             quantise_head(*turn_on_tensor(first, first + 1))
+        warm_up(WARM_AFTER)
         help_sweep((0, 1), (0,))
         for i in range(len(late_loads)):
             sort_late(i)

@@ -95,6 +95,7 @@ def tile_skew_preference_min_s10_kernel(tc, v, help_words, help_scales, truth_wo
         safe_planes = {h: sbuf([P, N_TILE], U8, "safe_planes%d_%d" % h) for h in halves}
 
         zeros = sbuf([P, 4 * WARM_WIDTH], BF16, "zeros")
+        table_warm = sbuf([P, 1], F32, "table_warm")
         zero_codes = sbuf([P, WARM_WIDTH], U32, "zero_codes")
         zero_planes = sbuf([P, WARM_WIDTH], U8, "zero_planes")
 
@@ -107,6 +108,7 @@ def tile_skew_preference_min_s10_kernel(tc, v, help_words, help_scales, truth_wo
         clear(help_later)
         clear(truth_planes)
         make_identity(nc, identity[:])
+        nc.scalar.activation(out=table_warm[:], in_=zeros[:, 0:2].bitcast(F32), func=SIGMOID)
 
         def load_units(raw, load):
             (m, g), (last_m, last_g) = load[0], load[-1]
@@ -191,8 +193,8 @@ def tile_skew_preference_min_s10_kernel(tc, v, help_words, help_scales, truth_wo
                 out=head_codes[:, first * P : last * P].bitcast(FP8X4), scales=head_planes[:, first * P : last * P], in_=grouped
             )
 
-        def sort_words(m, g):
-            nc.vector.tensor_copy(
+        def sort_words(copy, m, g):
+            copy(
                 out=v_sorted[m][:, WORDS * g : WORDS * (g + 1)].rearrange("p (s u i) -> p s u i", s=4, u=2),
                 in_=v_raw[m][:].bitcast(F32).rearrange("p (s g i u) -> p g s u i", s=4, g=GROUPS, u=2)[:, g],
             )
@@ -214,8 +216,10 @@ def tile_skew_preference_min_s10_kernel(tc, v, help_words, help_scales, truth_wo
                 in_=v_grouped[m][:, g * K_PASS : (g + 1) * K_PASS],
             )
 
-        def turn_on_vector(m):
-            for step in (sort_words, turn_squares, pair_words, quantise_v):
+        def turn_on_vector(sort, m):
+            for g in range(GROUPS):
+                sort_words(sort, m, g)
+            for step in (turn_squares, pair_words, quantise_v):
                 for g in range(GROUPS):
                     step(m, g)
 
@@ -344,13 +348,25 @@ def tile_skew_preference_min_s10_kernel(tc, v, help_words, help_scales, truth_wo
         for m in BY_TENSOR:
             for n in range(N_TILES):
                 truth_pass(m, n, 0)
-        for m in BY_VECTOR:
-            turn_on_vector(m)
+        sort_words(on_vector, 3, 0)
+        sort_words(on_vector, 3, 1)
+        turn_squares(3, 0)
+        turn_squares(3, 1)
+        pair_words(3, 0)
+        sort_words(on_vector, 3, 2)
+        quantise_v(3, 0)
+        pair_words(3, 1)
+        turn_squares(3, 2)
+        quantise_v(3, 1)
+        pair_words(3, 2)
+        quantise_v(3, 2)
+        turn_on_vector(on_vector, 4)
         for m in BY_TENSOR:
             for n in range(N_TILES):
                 truth_pass(m, n, 1)
                 truth_pass(m, n, 2)
                 keep_quality(m, n)
+        turn_on_vector(nc.scalar.copy, 5)
         help_sweep((3,), every_group)
         for n in range(N_TILES):
             for g in every_group:
@@ -381,10 +397,9 @@ def tile_skew_preference_min_s10_kernel(tc, v, help_words, help_scales, truth_wo
         for m in range(SWEEP):
             finish(*banks[m], m, 0, 0, N_TILE)
         last = M_TILES - 1
-        for m, n in [(m, 0) for m in range(SWEEP, M_TILES)] + [(m, 1) for m in range(last - 1)]:
+        for m, n in [(m, 0) for m in range(SWEEP, M_TILES)] + [(m, 1) for m in range(last)]:
             finish(*safety_tile(m, n), m, n, 0, N_TILE)
         keep_early(*safety_tile(last, 1), last, 1)
-        finish(*safety_tile(last - 1, 1), last - 1, 1, 0, N_TILE)
         for first in range(0, N_TILE, P):
             number, bank = take_bank()
             for g in every_group:

@@ -95,7 +95,6 @@ def tile_skew_preference_min_s10_kernel(tc, v, help_words, help_scales, truth_wo
         safe_planes = {h: sbuf([P, N_TILE], U8, "safe_planes%d_%d" % h) for h in halves}
 
         zeros = sbuf([P, 4 * WARM_WIDTH], BF16, "zeros")
-        table_warm = sbuf([P, 1], F32, "table_warm")
         zero_codes = sbuf([P, WARM_WIDTH], U32, "zero_codes")
         zero_planes = sbuf([P, WARM_WIDTH], U8, "zero_planes")
 
@@ -108,7 +107,6 @@ def tile_skew_preference_min_s10_kernel(tc, v, help_words, help_scales, truth_wo
         clear(help_later)
         clear(truth_planes)
         make_identity(nc, identity[:])
-        nc.scalar.activation(out=table_warm[:], in_=zeros[:, 0:2].bitcast(F32), func=SIGMOID)
 
         def load_units(raw, load):
             (m, g), (last_m, last_g) = load[0], load[-1]
@@ -121,8 +119,7 @@ def tile_skew_preference_min_s10_kernel(tc, v, help_words, help_scales, truth_wo
         def load_quarters(m):
             source = v[m * P : (m + 1) * P, :].rearrange("(j s) (g x) -> j (s g) x", s=4, g=GROUPS)
             for a in (0, 2, 1, 3):
-                queue = nc.sync if a < 2 else nc.scalar
-                queue.dma_start(
+                nc.sync.dma_start(
                     out=v_raw[m][32 * a : 32 * a + 32, :].rearrange("j (b x) -> j b x", x=P),
                     in_=source[:, :, a * P : (a + 1) * P],
                 )

@@ -25,7 +25,8 @@ N_TILE = 512
 N_TILES = N // N_TILE
 BANKS = 8
 BY_TENSOR = (0, 1, 2)
-BY_VECTOR = (3, 4, 5)
+MIDDLE = 3
+BY_VECTOR = (4, 5)
 MOVING_CODES_AT = 64
 STATIONARY_CODES_AT = 192
 STATIONARY_PLANES_AT = 128
@@ -78,12 +79,13 @@ def tile_skew_preference_min_s10_kernel(tc, v, help_words, help_scales, truth_wo
         head_grouped = sbuf([P, len(units) * K_PASS], BF16, "head_grouped")
         head_codes = shifted(len(units) * P, U32, "head_codes", STATIONARY_CODES_AT)
         head_planes = shifted(len(units) * P, U8, "head_planes", STATIONARY_PLANES_AT)
-        v_raw = {m: sbuf([P, K], BF16, "v_raw%d" % m) for m in BY_VECTOR}
-        v_sorted = {m: sbuf([P, K // 2], F32, "v_sorted%d" % m) for m in BY_VECTOR}
+        whole = (MIDDLE,) + BY_VECTOR
+        v_raw = {m: sbuf([P, K], BF16, "v_raw%d" % m) for m in whole}
+        v_sorted = {m: sbuf([P, K // 2], F32, "v_sorted%d" % m) for m in whole}
         v_turned = {m: sbuf([P, K // 2], F32, "v_turned%d" % m) for m in BY_VECTOR}
-        v_grouped = {m: sbuf([P, K], BF16, "v_grouped%d" % m) for m in BY_VECTOR}
-        v_codes = {m: shifted(GROUPS * P, U32, "v_codes%d" % m, STATIONARY_CODES_AT) for m in BY_VECTOR}
-        v_planes = {m: shifted(GROUPS * P, U8, "v_planes%d" % m, STATIONARY_PLANES_AT) for m in BY_VECTOR}
+        v_grouped = {m: sbuf([P, K], BF16, "v_grouped%d" % m) for m in whole}
+        v_codes = {m: shifted(GROUPS * P, U32, "v_codes%d" % m, STATIONARY_CODES_AT) for m in whole}
+        v_planes = {m: shifted(GROUPS * P, U8, "v_planes%d" % m, STATIONARY_PLANES_AT) for m in whole}
         halves = [(g, n) for g in range(GROUPS) for n in range(N_TILES)]
         safe_whole = [sbuf([P, 4, N], BF16, "safe_whole%d" % g) for g in range(GROUPS - 1)]
         safe_last = [sbuf([P, 4, N_TILE], BF16, "safe_last%d" % n) for n in range(N_TILES)]
@@ -152,6 +154,7 @@ def tile_skew_preference_min_s10_kernel(tc, v, help_words, help_scales, truth_wo
         load_help(2)
         load_truth(0)
         load_planes(truth_planes, truth_scales, TRUTH_PLANE_ROW, 0, GROUPS)
+        nc.sync.dma_start(out=v_raw[MIDDLE][:], in_=v[MIDDLE * P : (MIDDLE + 1) * P, :])
         load_truth(1)
         load_truth(2)
 
@@ -190,8 +193,8 @@ def tile_skew_preference_min_s10_kernel(tc, v, help_words, help_scales, truth_wo
                 out=head_codes[:, first * P : last * P].bitcast(FP8X4), scales=head_planes[:, first * P : last * P], in_=grouped
             )
 
-        def sort_words(copy, m, g):
-            copy(
+        def sort_words(m, g):
+            nc.vector.tensor_copy(
                 out=v_sorted[m][:, WORDS * g : WORDS * (g + 1)].rearrange("p (s u i) -> p s u i", s=4, u=2),
                 in_=v_raw[m][:].bitcast(F32).rearrange("p (s g i u) -> p g s u i", s=4, g=GROUPS, u=2)[:, g],
             )
@@ -213,12 +216,36 @@ def tile_skew_preference_min_s10_kernel(tc, v, help_words, help_scales, truth_wo
                 in_=v_grouped[m][:, g * K_PASS : (g + 1) * K_PASS],
             )
 
-        def turn_on_vector(sort, m):
-            for g in range(GROUPS):
-                sort_words(sort, m, g)
-            for step in (turn_squares, pair_words, quantise_v):
+        def turn_on_vector(m):
+            for step in (sort_words, turn_squares, pair_words, quantise_v):
                 for g in range(GROUPS):
                     step(m, g)
+
+        def turn_middle():
+            nc.vector.tensor_copy(
+                out=v_sorted[MIDDLE][:].rearrange("p (g u i) -> p g u i", g=GROUPS, u=2),
+                in_=v_raw[MIDDLE][:].bitcast(F32).rearrange("p (g i u) -> p g u i", g=GROUPS, u=2),
+            )
+            filled = []
+            for first, last in ((0, 2), (2, GROUPS)):
+                number, bank = take_bank()
+                for at in range(0, (last - first) * WORDS, P):
+                    words = v_sorted[MIDDLE][:, first * WORDS + at : first * WORDS + at + P]
+                    nc.tensor.transpose(bank[:, at : at + P], words, identity[:])
+                filled.append((number, bank, first, last))
+            for number, bank, first, last in filled:
+                count = last - first
+                grouped = v_grouped[MIDDLE][:, first * K_PASS : last * K_PASS]
+                nc.scalar.copy(
+                    out=grouped.bitcast(F32).rearrange("p (q r u) -> p q r u", q=count, u=2),
+                    in_=bank[:, 0 : count * WORDS].rearrange("p (q u r) -> p q r u", q=count, u=2),
+                )
+                free_banks.append(number)
+                nc.vector.quantize_mx(
+                    out=v_codes[MIDDLE][:, first * P : last * P].bitcast(FP8X4),
+                    scales=v_planes[MIDDLE][:, first * P : last * P],
+                    in_=grouped,
+                )
 
         def stationary(m, g):
             if m in BY_TENSOR:
@@ -330,9 +357,11 @@ def tile_skew_preference_min_s10_kernel(tc, v, help_words, help_scales, truth_wo
         help_sweep((0, 1), (0,))
         for i in range(len(late_loads)):
             sort_late(i)
-        turned = [turn_on_tensor(first, first + 2) for first in range(early_count, len(units), 2)]
+        turned = [turn_on_tensor(first, first + 2) for first in range(early_count, len(units) - 2, 2)]
+        help_sweep((2,), (0,))
         for bank in turned:
             quantise_head(*bank)
+        quantise_head(*turn_on_tensor(len(units) - 2, len(units)))
         for m in BY_VECTOR:
             load_quarters(m)
         for g in range(GROUPS - 1):
@@ -340,30 +369,21 @@ def tile_skew_preference_min_s10_kernel(tc, v, help_words, help_scales, truth_wo
         for n in range(N_TILES):
             load_safe(safe_last[n], GROUPS - 1, n * N_TILE, (n + 1) * N_TILE)
 
-        help_sweep((2,), (0,))
-        help_sweep(BY_TENSOR, (1, 2))
+        help_sweep((0, 1), (1, 2))
+        help_sweep((2,), (1, 2))
         for m in BY_TENSOR:
             for n in range(N_TILES):
                 truth_pass(m, n, 0)
-        sort_words(on_vector, 3, 0)
-        sort_words(on_vector, 3, 1)
-        turn_squares(3, 0)
-        turn_squares(3, 1)
-        pair_words(3, 0)
-        sort_words(on_vector, 3, 2)
-        quantise_v(3, 0)
-        pair_words(3, 1)
-        turn_squares(3, 2)
-        quantise_v(3, 1)
-        pair_words(3, 2)
-        quantise_v(3, 2)
-        turn_on_vector(on_vector, 4)
+        turn_middle()
+        for m in BY_VECTOR:
+            turn_on_vector(m)
         for m in BY_TENSOR:
             for n in range(N_TILES):
                 truth_pass(m, n, 1)
+        for m in BY_TENSOR:
+            for n in range(N_TILES):
                 truth_pass(m, n, 2)
                 keep_quality(m, n)
-        turn_on_vector(nc.scalar.copy, 5)
         help_sweep((3,), every_group)
         for n in range(N_TILES):
             for g in every_group:
@@ -397,10 +417,10 @@ def tile_skew_preference_min_s10_kernel(tc, v, help_words, help_scales, truth_wo
         for m, n in [(m, 0) for m in range(SWEEP, M_TILES)] + [(m, 1) for m in range(last)]:
             finish(*safety_tile(m, n), m, n, 0, N_TILE)
         keep_early(*safety_tile(last, 1), last, 1)
-        for first in range(0, N_TILE, P):
+        for first, width in ((0, 2 * P), (2 * P, P), (3 * P, P)):
             number, bank = take_bank()
             for g in every_group:
-                help_columns(bank, last, g, N_TILE + first, P)
+                help_columns(bank, last, g, N_TILE + first, width)
             for g in every_group:
-                truth_columns(bank, last, g, N_TILE + first, P)
-            finish(number, bank, last, 1, first, P)
+                truth_columns(bank, last, g, N_TILE + first, width)
+            finish(number, bank, last, 1, first, width)

@@ -70,7 +70,7 @@ def tile_skew_preference_min_s10_kernel(tc, v, help_words, help_scales, truth_wo
         help_codes = [shifted(2 * N, U8, "help_codes%d" % g, MOVING_CODES_AT) for g in range(GROUPS)]
         truth_codes = [shifted(4 * N, U8, "truth_codes%d" % g, MOVING_CODES_AT) for g in range(GROUPS)]
         early_loads = [[(0, 0)], [(1, 0), (2, 0)]]
-        late_loads = [[(m, 1), (m, 2)] for m in BY_TENSOR]
+        late_loads = [[(0, 1), (0, 2)], [(1, 1), (1, 2)], [(2, 1)], [(2, 2)]]
         units = [unit for load in early_loads + late_loads for unit in load]
         early_count = sum(len(load) for load in early_loads)
         early_raw = [sbuf([P, len(load) * K_PASS], BF16, "early_raw%d" % i) for i, load in enumerate(early_loads)]
@@ -147,15 +147,16 @@ def tile_skew_preference_min_s10_kernel(tc, v, help_words, help_scales, truth_wo
             load_units(raw, load)
         load_help(0)
         load_planes(help_first, help_scales, 0, 0, 1)
-        for raw, load in zip(late_raw, late_loads):
+        for raw, load in zip(late_raw[:-1], late_loads[:-1]):
             load_units(raw, load)
         load_help(1)
         load_planes(help_later, help_scales, 0, 1, GROUPS)
         load_help(2)
         load_truth(0)
         load_planes(truth_planes, truth_scales, TRUTH_PLANE_ROW, 0, GROUPS)
-        nc.sync.dma_start(out=v_raw[MIDDLE][:], in_=v[MIDDLE * P : (MIDDLE + 1) * P, :])
         load_truth(1)
+        load_units(late_raw[-1], late_loads[-1])
+        nc.sync.dma_start(out=v_raw[MIDDLE][:], in_=v[MIDDLE * P : (MIDDLE + 1) * P, :])
         load_truth(2)
 
         head_words = {}
@@ -167,31 +168,44 @@ def tile_skew_preference_min_s10_kernel(tc, v, help_words, help_scales, truth_wo
             for q, unit in enumerate(load):
                 head_words[unit] = [tile[:, WORDS * q + u * P : WORDS * q + (u + 1) * P] for u in range(2)]
 
+        for g in range(GROUPS):
+            head_words[(MIDDLE, g)] = [v_sorted[MIDDLE][:, WORDS * g + u * P : WORDS * g + (u + 1) * P] for u in range(2)]
+
         def sort_late(i):
             nc.vector.tensor_copy(
                 out=late_sorted[i][:].rearrange("p (q u i) -> p q u i", u=2, i=P),
                 in_=late_raw[i][:].bitcast(F32).rearrange("p (q i u) -> p q u i", u=2, i=P),
             )
 
-        def turn_on_tensor(first, last):
+        def grouped_of(unit):
+            m, g = unit
+            if m == MIDDLE:
+                return v_grouped[m][:, g * K_PASS : (g + 1) * K_PASS]
+            at = units.index(unit) * K_PASS
+            return head_grouped[:, at : at + K_PASS]
+
+        turned_at = {}
+
+        def turn_on_tensor(some):
             number, bank = take_bank()
-            for q, unit in enumerate(units[first:last]):
+            for q, unit in enumerate(some):
                 for u in range(2):
                     at = (2 * q + u) * P
                     nc.tensor.transpose(bank[:, at : at + P], head_words[unit][u], identity[:])
-            return number, bank, first, last
+                turned_at[unit] = (number, bank, q, some)
 
-        def quantise_head(number, bank, first, last):
-            count = last - first
-            grouped = head_grouped[:, first * K_PASS : last * K_PASS]
-            nc.scalar.copy(
-                out=grouped.bitcast(F32).rearrange("p (q r u) -> p q r u", q=count, u=2),
-                in_=bank[:, 0 : count * WORDS].rearrange("p (q u r) -> p q r u", q=count, u=2),
+        def pair_turned(copy, unit):
+            number, bank, q, some = turned_at.pop(unit)
+            copy(
+                out=grouped_of(unit).bitcast(F32).rearrange("p (r u) -> p r u", u=2),
+                in_=bank[:, q * WORDS : (q + 1) * WORDS].rearrange("p (u r) -> p r u", u=2),
             )
-            free_banks.append(number)
-            nc.vector.quantize_mx(
-                out=head_codes[:, first * P : last * P].bitcast(FP8X4), scales=head_planes[:, first * P : last * P], in_=grouped
-            )
+            if not any(other in turned_at for other in some):
+                free_banks.append(number)
+
+        def quantise_turned(unit):
+            codes, planes = stationary(*unit)
+            nc.vector.quantize_mx(out=codes.bitcast(FP8X4), scales=planes, in_=grouped_of(unit))
 
         def sort_words(m, g):
             nc.vector.tensor_copy(
@@ -221,31 +235,11 @@ def tile_skew_preference_min_s10_kernel(tc, v, help_words, help_scales, truth_wo
                 for g in range(GROUPS):
                     step(m, g)
 
-        def turn_middle():
+        def sort_middle():
             nc.vector.tensor_copy(
                 out=v_sorted[MIDDLE][:].rearrange("p (g u i) -> p g u i", g=GROUPS, u=2),
                 in_=v_raw[MIDDLE][:].bitcast(F32).rearrange("p (g i u) -> p g u i", g=GROUPS, u=2),
             )
-            filled = []
-            for first, last in ((0, 2), (2, GROUPS)):
-                number, bank = take_bank()
-                for at in range(0, (last - first) * WORDS, P):
-                    words = v_sorted[MIDDLE][:, first * WORDS + at : first * WORDS + at + P]
-                    nc.tensor.transpose(bank[:, at : at + P], words, identity[:])
-                filled.append((number, bank, first, last))
-            for number, bank, first, last in filled:
-                count = last - first
-                grouped = v_grouped[MIDDLE][:, first * K_PASS : last * K_PASS]
-                nc.scalar.copy(
-                    out=grouped.bitcast(F32).rearrange("p (q r u) -> p q r u", q=count, u=2),
-                    in_=bank[:, 0 : count * WORDS].rearrange("p (q u r) -> p q r u", q=count, u=2),
-                )
-                free_banks.append(number)
-                nc.vector.quantize_mx(
-                    out=v_codes[MIDDLE][:, first * P : last * P].bitcast(FP8X4),
-                    scales=v_planes[MIDDLE][:, first * P : last * P],
-                    in_=grouped,
-                )
 
         def stationary(m, g):
             if m in BY_TENSOR:
@@ -351,17 +345,20 @@ def tile_skew_preference_min_s10_kernel(tc, v, help_words, help_scales, truth_wo
             free_banks.append(number)
 
         warm_up(WARM_BEFORE)
-        for first in range(early_count):
-            quantise_head(*turn_on_tensor(first, first + 1))
+        for m in BY_TENSOR:
+            turn_on_tensor([(m, 0)])
+            pair_turned(nc.scalar.copy, (m, 0))
+            quantise_turned((m, 0))
         warm_up(WARM_AFTER)
         help_sweep((0, 1), (0,))
-        for i in range(len(late_loads)):
+        help_pass(2, 0, 0)
+        for i in range(len(late_loads) - 1):
             sort_late(i)
-        turned = [turn_on_tensor(first, first + 2) for first in range(early_count, len(units) - 2, 2)]
-        help_sweep((2,), (0,))
-        for bank in turned:
-            quantise_head(*bank)
-        quantise_head(*turn_on_tensor(len(units) - 2, len(units)))
+        for some in ([(0, 1)], [(0, 2), (1, 1)], [(1, 2), (2, 1)]):
+            turn_on_tensor(some)
+        for unit in ((0, 1), (1, 1), (2, 1), (0, 2), (1, 2)):
+            pair_turned(nc.scalar.copy, unit)
+            quantise_turned(unit)
         for m in BY_VECTOR:
             load_quarters(m)
         for g in range(GROUPS - 1):
@@ -369,18 +366,28 @@ def tile_skew_preference_min_s10_kernel(tc, v, help_words, help_scales, truth_wo
         for n in range(N_TILES):
             load_safe(safe_last[n], GROUPS - 1, n * N_TILE, (n + 1) * N_TILE)
 
-        help_sweep((0, 1), (1, 2))
-        help_sweep((2,), (1, 2))
-        for m in BY_TENSOR:
-            for n in range(N_TILES):
-                truth_pass(m, n, 0)
-        turn_middle()
+        help_pass(2, 1, 0)
+        help_sweep(BY_TENSOR, (1,))
+        help_sweep((0, 1), (2,))
+        for g in (0, 1):
+            for m in BY_TENSOR:
+                for n in range(N_TILES):
+                    truth_pass(m, n, g)
+        sort_late(len(late_loads) - 1)
+        sort_middle()
+        second_run = [(2, 2)] + [(MIDDLE, g) for g in range(GROUPS)]
+        turn_on_tensor(second_run[:2])
+        turn_on_tensor(second_run[2:])
+        for some in (second_run[:2], second_run[2:]):
+            for unit in some:
+                pair_turned(on_vector, unit)
+            for unit in some:
+                quantise_turned(unit)
         for m in BY_VECTOR:
             turn_on_vector(m)
         for m in BY_TENSOR:
-            for n in range(N_TILES):
-                truth_pass(m, n, 1)
-        for m in BY_TENSOR:
+            if m == 2:
+                help_sweep((2,), (2,))
             for n in range(N_TILES):
                 truth_pass(m, n, 2)
                 keep_quality(m, n)

@@ -33,6 +33,7 @@ STATIONARY_PLANES_AT = 128
 TRUTH_PLANE_ROW = 4
 SWEEP = 5
 SHARED = 256
+VECTOR_SHARE = 64
 WARM_WIDTH = 256
 WARM_BEFORE = 4
 WARM_AFTER = 2
@@ -171,10 +172,11 @@ def tile_skew_preference_min_s10_kernel(tc, v, help_words, help_scales, truth_wo
         for g in range(GROUPS):
             head_words[(MIDDLE, g)] = [v_sorted[MIDDLE][:, WORDS * g + u * P : WORDS * g + (u + 1) * P] for u in range(2)]
 
-        def sort_late(i):
+        def sort_late(i, q):
+            cols = slice(q * WORDS, (q + 1) * WORDS)
             nc.vector.tensor_copy(
-                out=late_sorted[i][:].rearrange("p (q u i) -> p q u i", u=2, i=P),
-                in_=late_raw[i][:].bitcast(F32).rearrange("p (q i u) -> p q u i", u=2, i=P),
+                out=late_sorted[i][:, cols].rearrange("p (u i) -> p u i", u=2),
+                in_=late_raw[i][:].bitcast(F32)[:, cols].rearrange("p (i u) -> p u i", u=2),
             )
 
         def grouped_of(unit):
@@ -351,9 +353,9 @@ def tile_skew_preference_min_s10_kernel(tc, v, help_words, help_scales, truth_wo
             quantise_turned((m, 0))
         warm_up(WARM_AFTER)
         help_sweep((0, 1), (0,))
-        help_pass(2, 0, 0)
         for i in range(len(late_loads) - 1):
-            sort_late(i)
+            for q in range(len(late_loads[i])):
+                sort_late(i, q)
         for some in ([(0, 1)], [(0, 2), (1, 1)], [(1, 2), (2, 1)]):
             turn_on_tensor(some)
         for unit in ((0, 1), (1, 1), (2, 1), (0, 2), (1, 2)):
@@ -366,14 +368,14 @@ def tile_skew_preference_min_s10_kernel(tc, v, help_words, help_scales, truth_wo
         for n in range(N_TILES):
             load_safe(safe_last[n], GROUPS - 1, n * N_TILE, (n + 1) * N_TILE)
 
-        help_pass(2, 1, 0)
+        help_sweep((2,), (0,))
         help_sweep(BY_TENSOR, (1,))
         help_sweep((0, 1), (2,))
         for g in (0, 1):
             for m in BY_TENSOR:
                 for n in range(N_TILES):
                     truth_pass(m, n, g)
-        sort_late(len(late_loads) - 1)
+        sort_late(len(late_loads) - 1, 0)
         sort_middle()
         second_run = [(2, 2)] + [(MIDDLE, g) for g in range(GROUPS)]
         turn_on_tensor(second_run[:2])
@@ -406,12 +408,14 @@ def tile_skew_preference_min_s10_kernel(tc, v, help_words, help_scales, truth_wo
         interleave_safe(nc.scalar.copy, 2, 0, SHARED, N_TILE)
         interleave_safe(on_vector, 2, 0, 0, SHARED)
         quantise_safe(1, 0)
+        quantise_safe(0, 1)
         quantise_safe(2, 0)
         quality_tile(5, 0)
         keep_quality(5, 0)
-        interleave_safe(nc.scalar.copy, 1, 1, 0, N_TILE)
+        interleave_safe(nc.scalar.copy, 1, 1, VECTOR_SHARE, N_TILE)
         interleave_safe(on_vector, 2, 1, 0, N_TILE)
-        for g in (0, 2, 1):
+        interleave_safe(on_vector, 1, 1, 0, VECTOR_SHARE)
+        for g in (2, 1):
             quantise_safe(g, 1)
 
         banks = [take_bank() for m in range(SWEEP)]

@@ -36,7 +36,7 @@ SHARED = 256
 VECTOR_SHARE = 64
 WARM_WIDTH = 256
 WARM_BEFORE = 4
-WARM_AFTER = 2
+WARM_AFTER = 3
 SAFE_ORDER = ((0, 1, 2), (0, 2, 1))
 
 
@@ -97,16 +97,18 @@ def tile_skew_preference_min_s10_kernel(tc, v, help_words, help_scales, truth_wo
         safe_codes = {h: shifted(N_TILE, U32, "safe_codes%d_%d" % h, MOVING_CODES_AT) for h in halves}
         safe_planes = {h: sbuf([P, N_TILE], U8, "safe_planes%d_%d" % h) for h in halves}
 
-        zeros = sbuf([P, 4 * WARM_WIDTH], BF16, "zeros")
+        zeros = sbuf([P, 128], BF16, "zeros")
         zero_codes = sbuf([P, WARM_WIDTH], U32, "zero_codes")
         zero_planes = sbuf([P, WARM_WIDTH], U8, "zero_planes")
 
         def clear(planes):
             nc.vector.memset(planes[:].rearrange("p g n -> p (g n)").bitcast(I32), 0)
 
-        nc.vector.memset(zeros[:].bitcast(I32), 0)
+        nc.vector.memset(zeros[:, 0:128].bitcast(I32), 0)
+        nc.vector.memset(zero_codes[:, 32:].bitcast(I32), 0)
+        nc.vector.memset(zero_planes[:, 32:].bitcast(I32), 0)
+        nc.vector.quantize_mx(out=zero_codes[:, 0:32].bitcast(FP8X4), scales=zero_planes[:, 0:32], in_=zeros[:, 0:128])
         clear(help_first)
-        nc.vector.quantize_mx(out=zero_codes[:].bitcast(FP8X4), scales=zero_planes[:], in_=zeros[:])
         clear(help_later)
         clear(truth_planes)
         make_identity(nc, identity[:])

from contextlib import ExitStack

import concourse.mybir as mybir
from concourse.masks import make_identity

M, K, N = 768, 1536, 1024
FLOPS = 3 * 2 * M * K * N

F32 = mybir.dt.float32
BF16 = mybir.dt.bfloat16
I32 = mybir.dt.int32
U32 = mybir.dt.uint32
U8 = mybir.dt.uint8
FP8X4 = mybir.dt.float8_e4m3fn_x4
FP4X4 = mybir.dt.float4_e2m1fn_x4
SIGMOID = mybir.ActivationFunctionType.Sigmoid
MIN = mybir.AluOpType.min

P = 128
K_PASS = 512
WORDS = K_PASS // 2
GROUPS = K // K_PASS
M_TILES = M // P
N_TILE = 512
N_TILES = N // N_TILE
BANKS = 8
BY_TENSOR = (0, 1, 2)
MIDDLE = 3
BY_VECTOR = (4, 5)
MOVING_CODES_AT = 64
STATIONARY_CODES_AT = 192
STATIONARY_PLANES_AT = 128
TRUTH_PLANE_ROW = 4
SWEEP = 5
SHARED = 256
VECTOR_SHARE = 64
WARM_WIDTH = 256
WARM_BEFORE = 4
WARM_AFTER = 3
SAFE_ORDER = ((0, 1, 2), (0, 2, 1))


def tile_skew_preference_min_s10_kernel(tc, v, help_words, help_scales, truth_words, truth_scales, safe, out):
    nc = tc.nc
    with ExitStack() as ctx:
        keep = ctx.enter_context(tc.tile_pool(name="keep", bufs=1))
        psum = ctx.enter_context(tc.psum_pool(name="psum", bufs=1))
        ctx.enter_context(tc.manual_schedule())

        def sbuf(shape, dtype, name):
            tile = keep.tile(shape, dtype, name=name, align_bytes=256)
            return tile

        def shifted(width, dtype, name, at):
            size = 1 if dtype == U8 else 4
            tile = sbuf([P, at // size + width], dtype, name)
            return tile[:, at // size :]

        free_banks = list(range(BANKS))

        def take_bank():
            number = free_banks.pop(0)
            tile = psum.tile([P, N_TILE], F32, name="bank%d" % number)
            return number, tile

        identity = sbuf([P, P], F32, "identity")
        help_first = sbuf([P, 1, N], U8, "help_first")
        help_later = sbuf([P, GROUPS - 1, N], U8, "help_later")
        help_planes = [help_first[:, 0, :]] + [help_later[:, g, :] for g in range(GROUPS - 1)]
        truth_planes = sbuf([P, GROUPS, N], U8, "truth_planes")
        help_codes = [shifted(2 * N, U8, "help_codes%d" % g, MOVING_CODES_AT) for g in range(GROUPS)]
        truth_codes = [shifted(4 * N, U8, "truth_codes%d" % g, MOVING_CODES_AT) for g in range(GROUPS)]
        early_loads = [[(0, 0)], [(1, 0), (2, 0)]]
        late_loads = [[(0, 1), (0, 2)], [(1, 1), (1, 2)], [(2, 1)], [(2, 2)]]
        units = [unit for load in early_loads + late_loads for unit in load]
        early_count = sum(len(load) for load in early_loads)
        early_raw = [sbuf([P, len(load) * K_PASS], BF16, "early_raw%d" % i) for i, load in enumerate(early_loads)]
        late_raw = [sbuf([P, len(load) * K_PASS], BF16, "late_raw%d" % i) for i, load in enumerate(late_loads)]
        late_sorted = [sbuf([P, len(load) * WORDS], F32, "late_sorted%d" % i) for i, load in enumerate(late_loads)]
        head_grouped = sbuf([P, len(units) * K_PASS], BF16, "head_grouped")
        head_codes = shifted(len(units) * P, U32, "head_codes", STATIONARY_CODES_AT)
        head_planes = shifted(len(units) * P, U8, "head_planes", STATIONARY_PLANES_AT)
        whole = (MIDDLE,) + BY_VECTOR
        v_raw = {m: sbuf([P, K], BF16, "v_raw%d" % m) for m in whole}
        v_sorted = {m: sbuf([P, K // 2], F32, "v_sorted%d" % m) for m in whole}
        v_turned = {m: sbuf([P, K // 2], F32, "v_turned%d" % m) for m in BY_VECTOR}
        v_grouped = {m: sbuf([P, K], BF16, "v_grouped%d" % m) for m in whole}
        v_codes = {m: shifted(GROUPS * P, U32, "v_codes%d" % m, STATIONARY_CODES_AT) for m in whole}
        v_planes = {m: shifted(GROUPS * P, U8, "v_planes%d" % m, STATIONARY_PLANES_AT) for m in whole}
        halves = [(g, n) for g in range(GROUPS) for n in range(N_TILES)]
        safe_whole = [sbuf([P, 4, N], BF16, "safe_whole%d" % g) for g in range(GROUPS - 1)]
        safe_last = [sbuf([P, 4, N_TILE], BF16, "safe_last%d" % n) for n in range(N_TILES)]
        safe_raw = {(g, n): safe_whole[g][:, :, n * N_TILE : (n + 1) * N_TILE] for g, n in halves[:-N_TILES]}
        for n in range(N_TILES):
            safe_raw[(GROUPS - 1, n)] = safe_last[n][:]
        safe_grouped = {h: sbuf([P, N_TILE, 4], BF16, "safe_grouped%d_%d" % h) for h in halves}
        safe_codes = {h: shifted(N_TILE, U32, "safe_codes%d_%d" % h, MOVING_CODES_AT) for h in halves}
        safe_planes = {h: sbuf([P, N_TILE], U8, "safe_planes%d_%d" % h) for h in halves}

        zeros = sbuf([P, 128], BF16, "zeros")
        zero_codes = sbuf([P, WARM_WIDTH], U32, "zero_codes")
        zero_planes = sbuf([P, WARM_WIDTH], U8, "zero_planes")

        def clear(planes):
            nc.vector.memset(planes[:].rearrange("p g n -> p (g n)").bitcast(I32), 0)

        nc.vector.memset(zeros[:, 0:128].bitcast(I32), 0)
        nc.vector.memset(zero_codes[:, 32:].bitcast(I32), 0)
        nc.vector.memset(zero_planes[:, 32:].bitcast(I32), 0)
        nc.vector.quantize_mx(out=zero_codes[:, 0:32].bitcast(FP8X4), scales=zero_planes[:, 0:32], in_=zeros[:, 0:128])
        clear(help_first)
        clear(help_later)
        clear(truth_planes)
        make_identity(nc, identity[:])

        def load_units(raw, load):
            (m, g), (last_m, last_g) = load[0], load[-1]
            rows = v[m * P : (last_m + 1) * P, g * K_PASS : (last_g + 1) * K_PASS]
            tiles = last_m + 1 - m
            nc.sync.dma_start(
                out=raw[:].rearrange("p (m x) -> p m x", m=tiles), in_=rows.rearrange("(m p) x -> p m x", p=P)
            )

        def load_quarters(m):
            source = v[m * P : (m + 1) * P, :].rearrange("(j s) (g x) -> j (s g) x", s=4, g=GROUPS)
            for a in (0, 2, 1, 3):
                nc.sync.dma_start(
                    out=v_raw[m][32 * a : 32 * a + 32, :].rearrange("j (b x) -> j b x", x=P),
                    in_=source[:, :, a * P : (a + 1) * P],
                )

        def load_planes(planes, scales, row, first, last):
            by_row = scales[first:last].bitcast(I32).rearrange("g (q r) n -> r q g n", r=4)
            for r in range(4):
                nc.sync.dma_start(out=planes[row + r : P : 32, :, :].bitcast(I32), in_=by_row[r])

        def load_help(g):
            nc.sync.dma_start(out=help_codes[g].bitcast(I32), in_=help_words[g].bitcast(I32))

        def load_truth(g):
            nc.sync.dma_start(
                out=truth_codes[g].bitcast(I32), in_=truth_words[g].rearrange("p n t -> p (n t)").bitcast(I32)
            )

        def load_safe(raw, g, first, last):
            rows = safe[g * K_PASS : (g + 1) * K_PASS, first:last]
            nc.sync.dma_start(out=raw[:], in_=rows.rearrange("(p t) n -> p t n", t=4))

        for raw, load in zip(early_raw, early_loads):
            load_units(raw, load)
        load_help(0)
        load_planes(help_first, help_scales, 0, 0, 1)
        for raw, load in zip(late_raw[:-1], late_loads[:-1]):
            load_units(raw, load)
        load_help(1)
        load_planes(help_later, help_scales, 0, 1, GROUPS)
        load_help(2)
        load_truth(0)
        load_planes(truth_planes, truth_scales, TRUTH_PLANE_ROW, 0, GROUPS)
        load_truth(1)
        load_units(late_raw[-1], late_loads[-1])
        nc.sync.dma_start(out=v_raw[MIDDLE][:], in_=v[MIDDLE * P : (MIDDLE + 1) * P, :])
        load_truth(2)

        head_words = {}
        for raw, load in zip(early_raw, early_loads):
            for q, unit in enumerate(load):
                words = raw[:].bitcast(F32)
                head_words[unit] = [words[:, WORDS * q + u : WORDS * (q + 1) : 2] for u in range(2)]
        for tile, load in zip(late_sorted, late_loads):
            for q, unit in enumerate(load):
                head_words[unit] = [tile[:, WORDS * q + u * P : WORDS * q + (u + 1) * P] for u in range(2)]

        for g in range(GROUPS):
            head_words[(MIDDLE, g)] = [v_sorted[MIDDLE][:, WORDS * g + u * P : WORDS * g + (u + 1) * P] for u in range(2)]

        def sort_late(i, q):
            cols = slice(q * WORDS, (q + 1) * WORDS)
            nc.vector.tensor_copy(
                out=late_sorted[i][:, cols].rearrange("p (u i) -> p u i", u=2),
                in_=late_raw[i][:].bitcast(F32)[:, cols].rearrange("p (i u) -> p u i", u=2),
            )

        def grouped_of(unit):
            m, g = unit
            if m == MIDDLE:
                return v_grouped[m][:, g * K_PASS : (g + 1) * K_PASS]
            at = units.index(unit) * K_PASS
            return head_grouped[:, at : at + K_PASS]

        turned_at = {}

        def turn_on_tensor(some):
            number, bank = take_bank()
            for q, unit in enumerate(some):
                for u in range(2):
                    at = (2 * q + u) * P
                    nc.tensor.transpose(bank[:, at : at + P], head_words[unit][u], identity[:])
                turned_at[unit] = (number, bank, q, some)

        def pair_turned(copy, unit):
            number, bank, q, some = turned_at.pop(unit)
            copy(
                out=grouped_of(unit).bitcast(F32).rearrange("p (r u) -> p r u", u=2),
                in_=bank[:, q * WORDS : (q + 1) * WORDS].rearrange("p (u r) -> p r u", u=2),
            )
            if not any(other in turned_at for other in some):
                free_banks.append(number)

        def quantise_turned(unit):
            codes, planes = stationary(*unit)
            nc.vector.quantize_mx(out=codes.bitcast(FP8X4), scales=planes, in_=grouped_of(unit))

        def sort_words(m, g):
            nc.vector.tensor_copy(
                out=v_sorted[m][:, WORDS * g : WORDS * (g + 1)].rearrange("p (s u i) -> p s u i", s=4, u=2),
                in_=v_raw[m][:].bitcast(F32).rearrange("p (s g i u) -> p g s u i", s=4, g=GROUPS, u=2)[:, g],
            )

        def turn_squares(m, g):
            cols = slice(WORDS * g, WORDS * (g + 1))
            nc.vector.transpose(out=v_turned[m][:, cols], in_=v_sorted[m][:, cols])

        def pair_words(m, g):
            nc.vector.tensor_copy(
                out=v_grouped[m][:, g * K_PASS : (g + 1) * K_PASS].bitcast(F32).rearrange("p (j h w) -> p h j w", h=2, w=4),
                in_=v_turned[m][:, WORDS * g : WORDS * (g + 1)].rearrange("p (h w j) -> p h j w", h=2, w=4),
            )

        def quantise_v(m, g):
            nc.vector.quantize_mx(
                out=v_codes[m][:, g * P : (g + 1) * P].bitcast(FP8X4),
                scales=v_planes[m][:, g * P : (g + 1) * P],
                in_=v_grouped[m][:, g * K_PASS : (g + 1) * K_PASS],
            )

        def turn_on_vector(m):
            for step in (sort_words, turn_squares, pair_words, quantise_v):
                for g in range(GROUPS):
                    step(m, g)

        def sort_middle():
            nc.vector.tensor_copy(
                out=v_sorted[MIDDLE][:].rearrange("p (g u i) -> p g u i", g=GROUPS, u=2),
                in_=v_raw[MIDDLE][:].bitcast(F32).rearrange("p (g i u) -> p g u i", g=GROUPS, u=2),
            )

        def stationary(m, g):
            if m in BY_TENSOR:
                at = units.index((m, g)) * P
                return head_codes[:, at : at + P], head_planes[:, at : at + P]
            return v_codes[m][:, g * P : (g + 1) * P], v_planes[m][:, g * P : (g + 1) * P]

        def interleave_safe(copy, g, n, first, last):
            copy(
                out=safe_grouped[(g, n)][:, first:last, :].rearrange("p (c i) t -> p c t i", i=4),
                in_=safe_raw[(g, n)][:, :, first:last].rearrange("p t (c i) -> p c t i", i=4),
            )

        def quantise_safe(g, n):
            nc.vector.quantize_mx(
                out=safe_codes[(g, n)].bitcast(FP8X4),
                scales=safe_planes[(g, n)][:],
                in_=safe_grouped[(g, n)][:].rearrange("p c t -> p (c t)"),
            )

        def mx_pass(acc, m, g, rhs, rhs_scale, start, stop):
            codes, planes = stationary(m, g)
            nc.tensor.matmul_mx(
                out=acc, lhsT=codes.bitcast(FP8X4), lhsT_scale=planes, rhs=rhs, rhs_scale=rhs_scale, start=start, stop=stop
            )

        quality_banks = {}

        def help_columns(bank, m, g, at, width):
            codes = help_codes[g][:, 2 * at : 2 * (at + width)].bitcast(FP4X4)
            mx_pass(bank[:, 0:width], m, g, codes, help_planes[g][:, at : at + width], g == 0, False)

        def truth_columns(bank, m, g, at, width):
            codes = truth_codes[g][:, 4 * at : 4 * (at + width)].bitcast(FP8X4)
            planes = truth_planes[TRUTH_PLANE_ROW:P, g, at : at + width]
            mx_pass(bank[:, 0:width], m, g, codes, planes, False, g == GROUPS - 1)

        def help_pass(m, n, g):
            if g == 0:
                quality_banks[(m, n)] = take_bank()
            help_columns(quality_banks[(m, n)][1], m, g, n * N_TILE, N_TILE)

        def truth_pass(m, n, g):
            truth_columns(quality_banks[(m, n)][1], m, g, n * N_TILE, N_TILE)

        def help_sweep(tiles, groups):
            for g in groups:
                for m in tiles:
                    for n in range(N_TILES):
                        help_pass(m, n, g)

        def quality_tile(m, n):
            for g in range(GROUPS):
                help_pass(m, n, g)
            for g in range(GROUPS):
                truth_pass(m, n, g)

        def safe_pass(bank, m, n, g):
            codes = safe_codes[(g, n)].bitcast(FP8X4)
            mx_pass(bank[:], m, g, codes, safe_planes[(g, n)][:], g == SAFE_ORDER[n][0], g == SAFE_ORDER[n][-1])

        def safety_tile(m, n):
            number, bank = take_bank()
            for g in SAFE_ORDER[n]:
                safe_pass(bank, m, n, g)
            return number, bank

        early = {}

        def keep_early(number, bank, m, n):
            kept = sbuf([P, N_TILE], F32, "early%d_%d" % (m, n))
            nc.scalar.activation(out=kept[:], in_=bank[:], func=SIGMOID)
            free_banks.append(number)
            early[(m, n)] = kept

        def keep_quality(m, n):
            keep_early(*quality_banks[(m, n)], m, n)

        def finish(number, bank, m, n, first, width):
            late = sbuf([P, width], F32, "late%d_%d_%d" % (m, n, first))
            nc.scalar.activation(out=late[:], in_=bank[:, 0:width], func=SIGMOID)
            free_banks.append(number)
            nc.vector.tensor_tensor(out=late[:], in0=late[:], in1=early[(m, n)][:, first : first + width], op=MIN)
            at = n * N_TILE + first
            nc.sync.dma_start(out=out[m * P : (m + 1) * P, at : at + width], in_=late[:])

        every_group = range(GROUPS)
        on_vector = nc.vector.tensor_copy


        def warm_up(count):
            number, bank = take_bank()
            for i in range(count):
                nc.tensor.matmul_mx(
                    out=bank[:, 0:WARM_WIDTH],
                    lhsT=zero_codes[:, 0:P].bitcast(FP8X4),
                    lhsT_scale=zero_planes[:, 0:P],
                    rhs=zero_codes[:].bitcast(FP8X4),
                    rhs_scale=zero_planes[:],
                    start=True,
                    stop=True,
                )
            free_banks.append(number)

        warm_up(WARM_BEFORE)
        for m in BY_TENSOR:
            turn_on_tensor([(m, 0)])
            pair_turned(nc.scalar.copy, (m, 0))
            quantise_turned((m, 0))
        warm_up(WARM_AFTER)
        help_sweep((0, 1), (0,))
        for i in range(len(late_loads) - 1):
            for q in range(len(late_loads[i])):
                sort_late(i, q)
        for some in ([(0, 1)], [(0, 2), (1, 1)], [(1, 2), (2, 1)]):
            turn_on_tensor(some)
        for unit in ((0, 1), (1, 1), (2, 1), (0, 2), (1, 2)):
            pair_turned(nc.scalar.copy, unit)
            quantise_turned(unit)
        for m in BY_VECTOR:
            load_quarters(m)
        for g in range(GROUPS - 1):
            load_safe(safe_whole[g], g, 0, N)
        for n in range(N_TILES):
            load_safe(safe_last[n], GROUPS - 1, n * N_TILE, (n + 1) * N_TILE)

        help_sweep((2,), (0,))
        help_sweep(BY_TENSOR, (1,))
        help_sweep((0, 1), (2,))
        for g in (0, 1):
            for m in BY_TENSOR:
                for n in range(N_TILES):
                    truth_pass(m, n, g)
        sort_late(len(late_loads) - 1, 0)
        sort_middle()
        second_run = [(2, 2)] + [(MIDDLE, g) for g in range(GROUPS)]
        turn_on_tensor(second_run[:2])
        turn_on_tensor(second_run[2:])
        for some in (second_run[:2], second_run[2:]):
            for unit in some:
                pair_turned(on_vector, unit)
            for unit in some:
                quantise_turned(unit)
        for m in BY_VECTOR:
            turn_on_vector(m)
        for m in BY_TENSOR:
            if m == 2:
                help_sweep((2,), (2,))
            for n in range(N_TILES):
                truth_pass(m, n, 2)
                keep_quality(m, n)
        help_sweep((3,), every_group)
        for n in range(N_TILES):
            for g in every_group:
                truth_pass(3, n, g)
            keep_quality(3, n)
        interleave_safe(nc.scalar.copy, 0, 1, 0, N_TILE)
        interleave_safe(on_vector, 0, 0, 0, N_TILE)
        for n in range(N_TILES):
            quality_tile(4, n)
            keep_quality(4, n)
        quantise_safe(0, 0)
        interleave_safe(on_vector, 1, 0, 0, N_TILE)
        interleave_safe(nc.scalar.copy, 2, 0, SHARED, N_TILE)
        interleave_safe(on_vector, 2, 0, 0, SHARED)
        quantise_safe(1, 0)
        quantise_safe(0, 1)
        quantise_safe(2, 0)
        quality_tile(5, 0)
        keep_quality(5, 0)
        interleave_safe(nc.scalar.copy, 1, 1, VECTOR_SHARE, N_TILE)
        interleave_safe(on_vector, 2, 1, 0, N_TILE)
        interleave_safe(on_vector, 1, 1, 0, VECTOR_SHARE)
        for g in (2, 1):
            quantise_safe(g, 1)

        banks = [take_bank() for m in range(SWEEP)]
        for g in SAFE_ORDER[0]:
            for m in range(SWEEP):
                safe_pass(banks[m][1], m, 0, g)
        for m in range(SWEEP):
            finish(*banks[m], m, 0, 0, N_TILE)
        last = M_TILES - 1
        for m, n in [(m, 0) for m in range(SWEEP, M_TILES)] + [(m, 1) for m in range(last)]:
            finish(*safety_tile(m, n), m, n, 0, N_TILE)
        keep_early(*safety_tile(last, 1), last, 1)
        for first, width in ((0, 2 * P), (2 * P, P), (3 * P, P)):
            number, bank = take_bank()
            for g in every_group:
                help_columns(bank, last, g, N_TILE + first, width)
            for g in every_group:
                truth_columns(bank, last, g, N_TILE + first, width)
            finish(number, bank, last, 1, first, width)
